import numpy as np, ml_dtypes
CORES = [6,15,38,47]
N = 4
BF = ml_dtypes.bfloat16
def gentries(a):
    return np.ascontiguousarray(a.reshape(8, 16, -1).transpose(0, 2, 1)).reshape(8, -1)
def gtable(e):
    e = np.asarray(e); return np.ascontiguousarray(e.reshape(8, -1, 16).transpose(0, 2, 1)).reshape(128, -1).astype(np.int32)
P, BS, T, CAP, G = 5376, 512, 3, 256, 128
S, SB, NEED, KILL = 2, 1, 9, 2
W = P + (N - 1) * G
def clans(rng, kk):
    sc = rng.choice(np.array([191.0, 120.0, 60.0], np.float32), (8, 1, 1)); cen = (sc * rng.random((8, 16, 4))).astype(np.float32); cen[:, :, 0] *= np.float32(0.1)
    t = np.maximum(1, (sc * (0.06 + 0.08 * rng.random((N, 8, 16, 1)))).astype(np.int32)); off = rng.integers(0, 4, (8, 1))
    def near():
        who = ((rng.random((N, 8, P)) * kk[:, None]).astype(np.int64) + off) & 3
        w = sc * (np.float32(0.05) + np.float32(0.15) * rng.random((N, 8, 1, P), dtype=np.float32))
        v = np.take_along_axis(np.broadcast_to(cen, (N, 8, 16, 4)), who[:, :, None, :], 3) + w * (2 * rng.random((N, 8, 16, P), dtype=np.float32) - 1)
        return np.clip(np.rint(v), 0, 191).astype(np.int32)
    x = near(); share = KILL * kk[:, None, None] * rng.choice(np.array([0.03, 0.06, 0.09]), (N, 8, 1, 1))
    y = np.where(rng.random((N, 8, 1, P)) < 0.1, 255, rng.integers(0, 192, (N, 8, 16, P), dtype=np.int32))
    return x, np.where(rng.random((N, 8, 1, P)) < share, near(), y), t
def chosen(key):
    return np.ascontiguousarray(np.argsort(key, axis=-1)[..., :16 * BS])
def deal(pts, num):
    a = np.empty((16, BS), np.int64); a[:, pts] = num.reshape(BS, 16).T
    return a.reshape(-1)
def parts(rng):
    x, y, t = clans(rng, rng.permutation(np.array([1, 1, 2, 2, 2, 3, 3, 4])))
    sd = rng.random((N, 8, BS)) < rng.choice(np.array([0.2, 0.4, 0.6, 0.9]), (N, 8, 1))
    c = chosen(rng.random((N, 8, T, S * W), dtype=np.float32))
    b = np.argsort(rng.random((N, 8, P)) * np.where(np.arange(P) < T * BS, 0.6, 1.0), axis=-1)[..., :(N - 1) * G]
    return x, y, t, sd, c, np.ascontiguousarray(b)
def pack(x, y, t, sd, c, b):
    c = c.reshape(N, 8, T, 16, BS).transpose(0, 1, 3, 2, 4).reshape(N, 128, T * BS)
    return {"x": x.reshape(N, 128, P).astype(np.float32).astype(BF), "y0": y.reshape(N, 128, P).astype(np.float32).astype(BF),
            "tl": t.reshape(N, 128, 1).astype(np.float32).astype(BF), "sd": sd.astype(np.float32).astype(BF),
            "cd": np.ascontiguousarray(c).astype(np.int32), "snd": np.stack([gtable(a) for a in b])}
def setup_inputs(rng):
    return pack(*parts(rng))
def setup_inputs_room(rng):
    x, y, t, sd, c, b = parts(rng)
    o = np.argsort(np.argsort(rng.random((N, 8, BS)), axis=-1), axis=-1); n = rng.choice(np.array([0, 1, CAP - 1, CAP, CAP + 1, BS]), (N, 8))
    n[0] = (CAP, CAP + 1, BS, CAP - 1, 1, 0, CAP, BS); n[1] = (BS, CAP, CAP + 1, CAP, CAP - 1, CAP, 0, 1)
    return pack(x, y, t, o < n[..., None], c, b)
def setup_inputs_ties(rng):
    x, y, t, sd, c, b = parts(rng)
    t = np.tile(rng.integers(0, 21, (1, 8, 16, 1)), (N, 1, 1, 1)); base = rng.integers(10, 121, (8, 16, 1))
    def step():
        return base + t * rng.integers(0, 3, (N, 8, 16, P), dtype=np.int32) + (rng.random((N, 8, 16, P), dtype=np.float32) < 0.3)
    x = step(); y = np.where(rng.random((N, 8, 1, P)) < 0.1 * KILL, step(), 255)
    t[:, 0] = 63; x[:, 0] = rng.choice(np.array([127, 128, 191]), (N, 16, P)); y[:, 0] = rng.choice(np.array([255, 255, 255, 191, 128, 64]), (N, 16, P))
    return pack(x, y, t, sd, c, b)
def setup_inputs_ends(rng):
    x, y, t, sd, c, b = parts(rng); a = np.arange(S * W); n = np.arange(BS); k = np.arange((N - 1) * G)
    key = rng.random((N, 8, T, S * W), dtype=np.float32)
    key[:, 1::2, :, S * P:] -= 1; key[:, 1::2, :, :S] -= 1; key[:, 1::2, :, S * (P - 1):S * P] -= 1
    key[:, 2] += (a >= 16 * BS).astype(np.float32); key[:, 4] += (a < S * W - 16 * BS).astype(np.float32)
    c = rng.permuted(chosen(key), axis=-1); c[:, 6] = np.arange(16 * BS)
    b[:, 1] = k; b[:, 3] = P - 1 - k; b[:, 7] = T * BS - (N - 1) * G + k
    sd[:, ::2] = n >= BS - CAP; sd[:, 1::2] = (n & 1) == 0; sd[:, 5] = (n == 0) | (n == BS - 1)
    return pack(x, y, t, sd, c, b)
def setup_inputs_dark(rng):
    x, y, t, sd, c, b = parts(rng); q = rng.permutation(N); g = rng.permutation(8)
    y[:, g[1]] = 255; t[:, g[2]] = 0
    for j in g[3:7]:
        x[:, j] = x[:, j] & 31; t[:, j] = 63
    y[:, g[3]] = y[:, g[3]] & 31; y[:, g[4]] = 128 + (y[:, g[4]] & 63)
    for r in range(N):
        m = np.isin(np.arange(BS) & 15, rng.permutation(16)[:16 * CAP // BS]); sd[r, g[4]] = m
        num = np.concatenate([rng.permutation(np.arange(S * P, S * W)), np.arange(16 * BS - S * (W - P))])
        c[r, g[4], 0] = deal(np.argsort(rng.random(BS) - m), num)
        m = rng.permutation(BS) < CAP; sd[r, g[5]] = m; o = rng.permutation(16)
        pl = np.argsort(o[np.arange(W) & 15] + rng.random(W))[:16 * CAP]; num = rng.permutation(S * pl + rng.integers(0, S, 16 * CAP))
        num = np.concatenate([num, rng.permutation(np.setdiff1d(np.arange(S * W), num))])[:16 * BS]
        c[r, g[5], 0] = deal(np.argsort(rng.random(BS) - m), num)
    c[:, g[4], 1:] = rng.permuted(np.tile(np.arange(16 * BS), (N, T - 1, 1)), axis=-1)
    key = rng.random((N, S * W)); key[:, S * BS:2 * S * BS] += 1; c[:, g[6], 0] = chosen(key)
    b[:, g[6]] = np.argsort(rng.random((N, P)) + (np.arange(P) // BS == 1), axis=-1)[:, :(N - 1) * G]
    sd[:, g[0]] = False; sd[q[0]] = False; sd[q[1], g[3]] = True
    return pack(x, y, t, sd, c, b)
def setup_inputs_spread(rng):
    x, y, t, sd, c, b = parts(rng)
    x = np.minimum((np.exp2(7.59 * rng.random((N, 8, 1, P))) * rng.random((N, 8, 16, P))).astype(np.int32), 191)
    y = np.minimum((np.exp2(7.59 * rng.random((N, 8, 1, P))) * rng.random((N, 8, 16, P))).astype(np.int32), 191)
    y = np.where(rng.random((N, 8, 1, P)) < rng.choice(np.array([0.1, 0.5, 0.9]), (N, 8, 1, 1)), 255, y)
    low = np.arange(16)[:, None] == rng.integers(0, 16, (N, 8, 1, P))
    y = np.where(rng.random((N, 8, 1, P)) < 0.15, np.where(low, y >> 3, 255), y)
    t = np.rint(np.exp2(6 * rng.random((N, 8, 16, 1)))).astype(np.int32) - 1
    return pack(x, y, np.minimum(t, 63), rng.random((N, 8, BS)) < rng.random((N, 8, 1)), c, b)
def check_inputs(d):
    bad = []
    for k, hi in (("x", 191), ("y0", 191), ("tl", 63), ("sd", 1)):
        v = np.asarray(d[k]).astype(np.float32); ok = (v >= 0) & (v <= hi) & (v == np.floor(v))
        if k == "y0": ok = ok | (v == 255)
        if not np.all(ok): bad.append("range of " + k)
    for k, hi in (("cd", S * W - 1), ("snd", P - 1)):
        if np.min(d[k]) < 0 or np.max(d[k]) > hi: bad.append("range of " + k)
    c = np.sort(np.asarray(d["cd"]).reshape(N, 8, 16, T, BS).transpose(0, 1, 3, 2, 4).reshape(N, 8, T, 16 * BS), axis=-1)
    if np.any(c[..., 1:] == c[..., :-1]): bad.append("equal numbers in a brood of cd")
    s = np.sort(np.stack([gentries(a) for a in d["snd"]]), axis=-1)
    if np.any(s[..., 1:] == s[..., :-1]): bad.append("equal numbers in snd")
    return bad
def windows(a, sl):
    res = []
    for r in range(N):
        w = [a[r]]
        for d in range(1, N):
            q = (r - d) % N; w.append(np.take_along_axis(a[q], sl[q, :, d - 1][:, None, :], 2))
        res.append(np.concatenate(w, axis=2))
    return np.stack(res)
def matches(come, xn, t):
    return np.add.reduce((np.abs(come - xn[:, None, :]) <= t[:, :, None]).astype(np.int64), axis=0) >= NEED
def reference(x, y0, tl, sd, cd, snd):
    X = x.astype(np.float32).astype(np.int32).reshape(N, 8, 16, P); Y = y0.astype(np.float32).astype(np.int32).reshape(N, 8, 16, P)
    t = tl.astype(np.float32).astype(np.int32).reshape(N, 8, 16, 1)
    C = (cd.astype(np.int64) >> SB).reshape(N, 8, 16, T * BS); sl = np.stack([gentries(a) for a in snd]).astype(np.int64).reshape(N, 8, N - 1, G)
    flag = np.zeros((N, 8, P), bool); flag[:, :, :BS] = sd.astype(np.float32) > 0.5; member = np.zeros((N, 8, P), bool)
    xw = windows(X, sl)
    for s in range(T):
        fl = flag[:, :, s * BS:(s + 1) * BS]
        member[:, :, s * BS:(s + 1) * BS] = fl & (np.add.accumulate(fl.astype(np.int64), axis=2) <= CAP)
        new = np.zeros((N, 8, W), bool)
        for r in range(N):
            for g in range(8):
                n = np.flatnonzero(member[r, g, s * BS:(s + 1) * BS]) + s * BS; c = C[r, g][:, n]
                come = xw[r, g][:, c.reshape(-1)].reshape(16, 16, len(n))
                new[r, g][c[matches(come, X[r, g][:, n], t[r, g])]] = True
        for r in range(N):
            flag[r] |= new[r, :, :P]
            for d in range(1, N):
                q = (r - d) % N
                for g in range(8): flag[q, g, sl[q, g, d - 1][new[r, g, P + (d - 1) * G:P + d * G]]] = True
    for s in range(T - 1, -1, -1):
        yw = windows(Y, sl); Z = Y.copy()
        for r in range(N):
            for g in range(8):
                n = np.flatnonzero(member[r, g, s * BS:(s + 1) * BS]) + s * BS; c = C[r, g][:, n]; xn = X[r, g][:, n]
                come = yw[r, g][:, c.reshape(-1)].reshape(16, 16, len(n))
                dead = np.add.reduce(matches(come, xn, t[r, g]).astype(np.int64), axis=0) >= KILL
                Z[r, g][:, n] = np.where(dead, 255, (xn + np.minimum(191, np.minimum.reduce(come, axis=1))) >> 1)
        Y = Z
    return {"yv": np.ascontiguousarray(Y[:, :, :, :T * BS]).reshape(N, 128, T * BS).astype(np.float32).astype(BF), "yf": np.where(member, 2, flag.astype(np.int64)).astype(np.float32).astype(BF)}

@@ -1,0 +1,510 @@
+from concourse.bass import DstId, RemoteDMATransfer
+from concourse.mybir import AluOpType as OP, ActivationFunctionType as AF
+
+P, PL, NB, BS, CAP, BK = 5376, 5760, 384, 512, 256, 128
+ST = 2 * PL
+WW = ST + 1024
+BIG = 1023.0
+YO = CAP
+
+SCRATCH = {
+    "xw": ("sbuf", [128, PL], "bfloat16"),
+    "ya": ("sbuf", [128, YO + PL], "bfloat16"), "yb": ("sbuf", [128, YO + PL], "bfloat16"),
+    "cdt": ("sbuf", [128, 1536], "int32"), "comp": ("sbuf", [128, 1024], "int32"),
+    "snd32": ("sbuf", [128, 24], "int32"), "snd16": ("sbuf", [128, 24], "uint16"), "snd2": ("sbuf", [128, 24], "uint16"),
+    "snd2i": ("sbuf", [128, 24], "int32"),
+    "ci": ("sbuf", [128, 256], "int32"), "xi": ("sbuf", [128, 256], "int32"), "vt": ("sbuf", [128, 256], "int32"),
+    "cf": ("sbuf", [128, 4096], "bfloat16"), "cb": ("sbuf", [128, 4096], "bfloat16"),
+    "d0": ("sbuf", [128, 1024], "bfloat16"), "mt": ("sbuf", [128, 256], "bfloat16"),
+    "ai": ("sbuf", [128, 256], "int32"), "hi": ("sbuf", [128, 256], "int32"), "d255": ("sbuf", [128, 256], "float32"),
+    "nm": ("sbuf", [128, 256], "float32"), "vo": ("sbuf", [128, 256], "uint16"), "trash": ("sbuf", [128, 64], "float32"),
+    "w1": ("sbuf", [128, WW], "bfloat16"), "w2": ("sbuf", [128, WW], "float32"),
+    "ones": ("sbuf", [128, 1024], "bfloat16"), "cst": ("sbuf", [128, 1024], "float32"),
+    "C": ("sbuf", [128, 2048], "bfloat16"), "R": ("sbuf", [128, 2048], "bfloat16"),
+    "ident": ("sbuf", [128, 128], "bfloat16"), "B": ("sbuf", [128, 128], "bfloat16"), "A1": ("sbuf", [128, 128], "bfloat16"),
+    "sdrep": ("sbuf", [128, 512], "bfloat16"), "sdblk": ("sbuf", [128, 336], "bfloat16"),
+    "L0": ("sbuf", [128, 400], "bfloat16"), "L1": ("sbuf", [128, 400], "bfloat16"), "L2": ("sbuf", [128, 400], "bfloat16"),
+    "Lg": ("sbuf", [128, 512], "bfloat16"), "fsend": ("sbuf", [128, NB], "bfloat16"),
+    "xsend": ("sbuf", [128, NB], "bfloat16"), "ysend": ("sbuf", [128, NB], "bfloat16"),
+    "bw": ("sbuf", [128, P], "bfloat16"), "io384": ("sbuf", [128, NB], "bfloat16"), "binv": ("sbuf", [128, 64], "uint16"),
+    "c2b": ("sbuf", [128, 768], "bfloat16"), "c2w": ("sbuf", [128, 1024], "bfloat16"),
+    "tlb": ("sbuf", [128, 1], "bfloat16"), "warm": ("sbuf", [128, 8], "float32"),
+    "flw": ("sbuf", [128, 32], "bfloat16"), "one32": ("sbuf", [128, 32], "float32"), "sc32": ("sbuf", [128, 32], "float32"),
+    "pp": ("sbuf", [128, 32], "float32"), "sl": ("sbuf", [128, 32], "float32"), "sl16": ("sbuf", [128, 32], "uint16"),
+    "zz": ("sbuf", [128, 32], "float32"), "t512": ("sbuf", [128, 32], "float32"),
+    "itp": ("sbuf", [128, 64], "int32"), "it2": ("sbuf", [128, 64], "int32"), "it3": ("sbuf", [128, 32], "int32"),
+    "mw": ("sbuf", [128, CAP + 1536], "bfloat16"), "memrep": ("sbuf", [128, 1536], "bfloat16"),
+    "memblk": ("sbuf", [128, 336], "bfloat16"), "w1blk": ("sbuf", [128, 672], "bfloat16"),
+    "w2blk": ("sbuf", [128, 672], "float32"), "w2bb": ("sbuf", [128, 672], "bfloat16"),
+    "tmpR": ("sbuf", [128, NB], "bfloat16"), "yfl": ("sbuf", [128, 336], "float32"), "yfb": ("sbuf", [128, 336], "bfloat16"),
+    "psd0": ("psum", [128, 1024], "float32"), "psd1": ("psum", [128, 1024], "float32"),
+    "cnt0": ("psum", [128, 512], "float32"), "cnt1": ("psum", [128, 512], "float32"),
+    "psA": ("psum", [128, 512], "float32"), "psB": ("psum", [128, 512], "float32"),
+}
+for _s in range(3):
+    SCRATCH["c16_%d" % _s] = ("sbuf", [128, 256], "uint16")
+    SCRATCH["xm%d" % _s] = ("sbuf", [128, 256], "bfloat16")
+    SCRATCH["xT%d" % _s] = ("sbuf", [128, 256], "bfloat16")
+    SCRATCH["sb16_%d" % _s] = ("sbuf", [128, 32], "uint16")
+    SCRATCH["vs%d" % _s] = ("sbuf", [128, 32], "float32")
+    SCRATCH["ab%d" % _s] = ("sbuf", [128, 1024], "bfloat16")
+    SCRATCH["nr%d" % _s] = ("sbuf", [128, 1024], "bfloat16")
+for _s in range(2):
+    SCRATCH["scn%d" % _s] = ("sbuf", [128, 1024], "bfloat16")
+
+_EX = ["x", "f0", "y", "f1", "b2", "f2", "b1"]
+_DM = ["snd", "xa", "xb", "tl", "sd", "cd0", "cd1", "sk", "ya", "yb", "bl1", "bl2", "blm", "cy", "o2", "o1", "o0", "of"]
+SEMAPHORES = ["qv", "qs", "qt", "qg"] + ["ls_" + e for e in _EX] + ["rs_" + e for e in _EX] + ["d_" + d for d in _DM]
+
+
+def rank_program(g, core, T, topo):
+    rank = T.rank_of(core)
+    if rank is None:
+        return
+    nr_ranks = len(T.cores)
+    eng = {"v": g.vector, "s": g.scalar, "t": g.tensor, "g": g, "y": g.sync}
+    known = {q: {} for q in eng}
+    clock = {}
+    total = {}
+    recs = {}
+
+    def width(n):
+        return SCRATCH[n][1][1]
+
+    def reg(r):
+        return r[0], (r[1] if len(r) > 1 else 0), (r[2] if len(r) > 2 else width(r[0]))
+
+    def is_ps(n):
+        return SCRATCH[n][0] == "psum"
+
+    def ap(r):
+        n, a, b = reg(r)
+        if len(r) > 3:
+            return T[n][:, a:b:r[3]]
+        return T[n][:, a:b]
+
+    def need(q, evs):
+        best = {}
+        for sem, n in evs:
+            if known[q].get(sem, 0) < n and best.get(sem, 0) < n:
+                best[sem] = n
+        for sem in list(best):
+            n = best[sem]
+            if any(o != sem and clock[(o, m)].get(sem, 0) >= n for o, m in best.items()):
+                del best[sem]
+        for sem, n in best.items():
+            eng[q].wait_ge(T.sem[sem], n)
+            for k, m in clock[(sem, n)].items():
+                if known[q].get(k, 0) < m:
+                    known[q][k] = m
+
+    def deps(q, R, W):
+        evs = []
+        for r, w in [(r, is_ps(r[0])) for r in R] + [(r, True) for r in W]:
+            n, a, b = reg(r)
+            if is_ps(n):
+                a, b = 0, width(n)
+            for c0, c1, iw, qq, ev in recs.get(n, []):
+                if c0 < b and a < c1 and (w or iw) and not (q == "t" and qq == "t"):
+                    evs.append(ev)
+        return evs
+
+    def note(q, R, W, ev):
+        for r in W:
+            n, a, b = reg(r)
+            if is_ps(n):
+                a, b = 0, width(n)
+            if len(r) <= 3 and not is_ps(n):
+                recs[n] = [e for e in recs.get(n, []) if not (a <= e[0] and e[1] <= b)]
+            elif is_ps(n):
+                recs[n] = [e for e in recs.get(n, []) if q == "t" and e[3] == "t"]
+            recs.setdefault(n, []).append((a, b, True, q, ev))
+        for r in R:
+            n, a, b = reg(r)
+            if is_ps(n):
+                recs[n] = [(0, width(n), True, q, ev)]
+            else:
+                recs.setdefault(n, []).append((a, b, False, q, ev))
+
+    def event(q, sem, n):
+        total[sem] = total.get(sem, 0) + n
+        ev = (sem, total[sem])
+        clock[ev] = dict(known[q])
+        clock[ev][sem] = total[sem]
+        return ev
+
+    def op(q, fn, R, W):
+        need(q, deps(q, R, W))
+        sem = "q" + q
+        fn().then_inc(T.sem[sem], 1)
+        note(q, R, W, event(q, sem, 1))
+
+    def dma(q, name, pairs, R, W):
+        need(q, deps(q, R, W))
+        for o, i in pairs:
+            eng[q].dma_start(o, i).then_inc(T.sem["d_" + name], 16)
+        note(q, R, W, event(q, "d_" + name, 16 * len(pairs)))
+
+    def tc(q, o, i):
+        if q == "v":
+            op("v", lambda: g.vector.tensor_copy(ap(o), ap(i)), [i], [o])
+        else:
+            op("s", lambda: g.scalar.activation(ap(o), ap(i), AF.Copy), [i], [o])
+
+    def gat(q, o, win, off):
+        if q == "v":
+            op("v", lambda: g.vector.tensor_copy(ap(o), ap(win).indirect(ap(off))), [win, off], [o])
+        else:
+            op("s", lambda: g.scalar.activation(ap(o), ap(win).indirect(ap(off)), AF.Copy), [win, off], [o])
+
+    def sca(win, off, i):
+        op("v", lambda: g.vector.tensor_copy(ap(win).indirect(ap(off)), ap(i)), [i, off], [win])
+
+    def tt(o, a, b, f):
+        op("v", lambda: g.vector.tensor_tensor(ap(o), ap(a), ap(b), f), [a, b], [o])
+
+    def ts(o, a, s1, f1, s2=None, f2=None):
+        if f2 is None:
+            op("v", lambda: g.vector.tensor_scalar(ap(o), ap(a), s1, None, f1), [a], [o])
+        else:
+            op("v", lambda: g.vector.tensor_scalar(ap(o), ap(a), s1, s2, f1, f2), [a], [o])
+
+    def fill(o, c):
+        op("v", lambda: g.vector.memset(ap(o), c), [], [o])
+
+    def mm(o, l, r, start, stop):
+        op("t", lambda: g.tensor.matmul(ap(o), ap(l), ap(r), start, stop), [l, r], [o])
+
+    def sel(o, i, pattern, cmp, fl, base, cm):
+        op("g", lambda: g.affine_select(ap(o), ap(i), pattern, cmp, fl, base, cm), [i], [o])
+
+    def iota(o, pattern, base, cm):
+        if SCRATCH[o[0]][2] == "int32":
+            op("g", lambda: g.iota(ap(o), pattern, base, cm), [], [o])
+        else:
+            op("g", lambda: g.iota(ap(o), pattern, base, cm, allow_small_or_imprecise_dtypes=True), [], [o])
+
+    def send(name, src, dst, col, sign):
+        need("g", deps("g", [(src,)], []))
+        trs, cnt, at = [], 0, 0
+        for d in range(1, nr_ranks):
+            to = T.cores[(rank + sign * d) % nr_ranks]
+            es = topo.engines(core, to)
+            n = len(es) // 4
+            a, b = topo.chip(core), topo.chip(to)
+            if topo.mates(a, b) or topo.same_plane(a, b):
+                mine = es[at:at + n]
+                at += n
+            else:
+                mine = es[2 * n:]
+            rid, pid, _ = topo.addr(to)
+            c0 = col + (d - 1) * BK
+            trs.append(RemoteDMATransfer(dst_ids=[DstId(rid=rid, pnc=pid)], dma_engine_mask=sum(1 << e for e in mine),
+                                         remote_sem=T.sem["rs_" + name], src=T[src][:, (d - 1) * BK:d * BK],
+                                         dst=T[dst][:, c0:c0 + BK]))
+            cnt += len(mine)
+        g.remote_dma_fused(trs, local_sem=T.sem["ls_" + name])
+        note("g", [(src,)], [], event("g", "ls_" + name, cnt))
+        total["rs_" + name] = cnt
+        ev = ("rs_" + name, cnt)
+        clock[ev] = {"rs_" + name: cnt}
+        recs.setdefault(dst, [])
+        recs[dst] = [e for e in recs[dst] if not (col <= e[0] and e[1] <= col + NB)]
+        recs[dst].append((col, col + NB, True, "r", ev))
+        return ev
+
+    def cmat(r):
+        return ("C", 128 * r, 128 * r + 128)
+
+    h = P // 2
+    dma("y", "snd", [(T.snd32[:, :], T.snd[:, :])], [], [("snd32",)])
+    dma("y", "xa", [(T.xw[:, 0:h], T.x[:, 0:h])], [], [("xw", 0, h)])
+    dma("s", "xb", [(T.xw[:, h:P], T.x[:, h:P])], [], [("xw", h, P)])
+    fill(("sdrep",), 0.0)
+    fill(("ones",), 1.0)
+    fill(("R",), -1.0)
+    fill(("sdblk",), 0.0)
+    fill(("C",), 0.0)
+    dma("y", "sd", [(T.sdrep[0::16, :], T.sd[:, :])], [], [("sdrep",)])
+    dma("y", "cd0", [(T.cdt[:, 0:BS], T.cd[:, 0:BS])], [], [("cdt", 0, BS)])
+    dma("y", "tl", [(T.tlb[:, :], T.tl[:, :])], [], [("tlb",)])
+    dma("y", "sk", [(T.sdblk[0::16, :], T.sd[:, 0:336]), (T.sdblk[1::16, 0:BS - 336], T.sd[:, 336:BS])], [], [("sdblk",)])
+    dma("y", "cd1", [(T.cdt[:, BS:3 * BS], T.cd[:, BS:3 * BS])], [], [("cdt", BS, 3 * BS)])
+
+    sel(("B",), ("ones", 0, 128), [[-16, 8], [0, 16]], OP.is_ge, 0.0, 0, 1)
+    sel(("B",), ("B",), [[16, 8], [0, 16]], OP.is_ge, 0.0, 15, -1)
+    sel(("A1",), ("R", 0, 128), [[16, 8], [0, 16]], OP.is_ge, 0.0, 15, -1)
+    sel(("A1",), ("A1",), [[-1, 128]], OP.is_gt, 0.0, 0, 1)
+    sel(("A1",), ("A1",), [[-1, 128]], OP.not_equal, -(BIG + 1), 0, 1)
+    iota(("itp",), [[0, 64]], 0, 1)
+    iota(("it3",), [[16, 32]], BS, 0)
+    iota(("it2",), [[16, 64]], ST, 0)
+    sel(("ident",), ("ones", 0, 128), [[-1, 128]], OP.is_equal, 0.0, 0, 1)
+
+    op("s", lambda: g.scalar.activation(ap(("warm",)), ap(("ones", 0, 8)), AF.Sigmoid), [("ones", 0, 8)], [("warm",)])
+    for a in range(0, ST, 1024):
+        b = min(ST, a + 1024)
+        op("s", lambda a=a, b=b: g.scalar.activation(ap(("w2", a, b)), ap(("ones", 0, b - a)), AF.Copy, scale=0.0),
+           [("ones", 0, b - a)], [("w2", a, b)])
+
+    for q in range(8):
+        tc("v", ("C", 16 * q, 16 * q + 129 * 15 + 1, 129), ("B", 16 * q, 16 * q + 16))
+    tc("v", ("snd16",), ("snd32",))
+    fill(("one32",), 1.0)
+    ts(("itp",), ("itp",), 15, OP.bitwise_and)
+    tt(("t512",), ("it3",), ("itp", 0, 32), OP.add)
+    tt(("trash",), ("it2",), ("itp",), OP.add)
+    for s in range(3):
+        ts(("vs%d" % s,), ("t512",), float(512 * s - 256), OP.add)
+    fill(("w1", 0, ST), 0.0)
+    fill(("comp", 0, CAP), 255)
+
+    gat("v", ("xsend",), ("xw", 0, P), ("snd16",))
+    send("x", "xsend", "xw", P, 1)
+    sel(("R",), ("R",), [[-1, 128], [0, 16]], OP.is_equal, 0.0, 0, 1)
+    iota(("io384",), [[1, NB]], -NB // 2, 0)
+
+    def pack(s):
+        r = ("cdt", BS * s, BS * s + BS)
+        ts(r, r, 256, OP.mult)
+        tt(r, r, ("xw", BS * s, BS * s + BS), OP.add)
+
+    def lists(s):
+        ts(("flw",), ("psA", 0, 32), 0.25, OP.is_gt)
+        mm(("psB", 0, 32), ("B",), ("flw",), True, True)
+        mm(("psB", 32, 64), ("A1",), ("flw",), True, True)
+        op("v", lambda: g.vector.tensor_tensor_scan(ap(("sc32",)), ap(("one32",)), ap(("psB", 0, 32)), BIG, OP.mult, OP.add),
+           [("one32",), ("psB", 0, 32)], [("sc32",)])
+        tt(("pp",), ("psB", 32, 64), ("sc32",), OP.add)
+        tt(("sl",), ("pp",), ("t512",), OP.min)
+        tc("v", ("sl16",), ("sl",))
+        sca(("comp",), ("sl16",), ("cdt", BS * s, BS * s + BS))
+        m = ("comp", 0, CAP)
+        ts(("ci",), m, 9, OP.arith_shift_right)
+        tc("v", ("c16_%d" % s,), ("ci",))
+        ts(("xi",), m, 255, OP.bitwise_and)
+        tc("v", ("xm%d" % s,), ("xi",))
+        for k in range(2):
+            mm(("psA", 128 * k, 128 * k + 128), ("xm%d" % s, 128 * k, 128 * k + 128), ("ident",), True, True)
+
+    def take_xt(s):
+        tc("s", ("xT%d" % s,), ("psA", 0, 256))
+
+    def slots(s):
+        ts(("vt",), ("comp", 0, CAP), 8, OP.arith_shift_right)
+        ts(("zz",), ("pp",), 255.5, OP.is_gt, 8192.0, OP.mult)
+        tt(("zz",), ("pp",), ("zz",), OP.add)
+        tt(("zz",), ("zz",), ("vs%d" % s,), OP.min)
+        tc("v", ("sb16_%d" % s,), ("zz",))
+
+    def members(s):
+        gat("s", ("memrep", BS * s, BS * s + BS), ("mw",), ("sb16_%d" % s,))
+
+    def match(s, wn, w0, cand, split, post, hook, fresh):
+        win = (wn, w0, w0 + PL)
+        off = "c16_%d" % s
+
+        def G(c):
+            k, j = 64 * c, 1024 * c
+            gat("s", (cand, j + 16 * split, j + 1024), win, (off, k + split, k + 64))
+            gat("v", (cand, j, j + 16 * split), win, (off, k, k + split))
+
+        def X(c):
+            ps, hf = "psd%d" % (c % 2), c // 2
+            for b in range(2):
+                q = (2 * c + b) % 4
+                mm((ps, 512 * b, 512 * b + 512), ("xT%d" % s, 128 * hf, 128 * hf + 128), ("R", 512 * q, 512 * q + 512), True, False)
+            for b in range(2):
+                j = 1024 * c + 512 * b
+                mm((ps, 512 * b, 512 * b + 512), ("ident",), (cand, j, j + 512), False, True)
+
+        def Ab(c):
+            o, i = ("ab%d" % (c % 3),), ("psd%d" % (c % 2),)
+            op("s", lambda: g.scalar.activation(ap(o), ap(i), AF.Abs), [i], [o])
+
+        def Le(c):
+            o, i = ("nr%d" % (c % 3),), ("ab%d" % (c % 3),)
+            op("v", lambda: g.vector.tensor_scalar(ap(o), ap(i), ap(("tlb",)), None, OP.is_le), [i, ("tlb",)], [o])
+
+        def Ct(c):
+            k = 64 * (c // 2)
+            for i in range(16):
+                mm(("cnt%d" % (c % 2), k, k + 64), cmat(i), ("nr%d" % (c % 3), i, 1024, 16), i == 0, i == 15)
+
+        def Po(c):
+            k = 64 * (c // 2)
+            post(c, ("cnt%d" % (c % 2), k, k + 64))
+
+        def hk(n):
+            if n in hook:
+                hook[n]()
+
+        G(0)
+        if fresh:
+            take_xt(s)
+        G(1); X(0); Ab(0); G(2); hk("g2"); X(1); Le(0); Ab(1); G(3); hk("g3"); Ct(0); X(2); Le(1); Ab(2); Po(0); hk("p0")
+        Ct(1); X(3); Le(2); Ab(3); Po(1); hk("p1"); Ct(2); Le(3); hk("l3"); Po(2); Ct(3); Po(3)
+
+    def fwd_match(s, hook, fresh):
+        def post(c, cn):
+            r = (64 * c, 64 * c + 64)
+            nm = ("nm",) + r
+            ts(nm, cn, 8.5, OP.is_lt, 30000.0, OP.mult)
+            tt(nm, nm, ("trash",), OP.min)
+            tt(nm, nm, ("vt",) + r, OP.max)
+            tc("v", ("vo",) + r, nm)
+        match(s, "xw", 0, "cf", 40, post, hook, fresh)
+
+    def scatter_s(c):
+        w, o = ("w2",), ("vo", 64 * c, 64 * c + 64)
+        op("s", lambda: g.scalar.activation(ap(w).indirect(ap(o)), ap(("cst",)), AF.Sigmoid), [o, ("cst",)], [w])
+
+    def scatter_v(c):
+        sca(("w1",), ("vo", 64 * c, 64 * c + 64), ("ones",))
+
+    def flags_out(s):
+        scatter_s(0); scatter_s(1); scatter_v(2); scatter_v(3)
+        tc("s", ("c2b",), ("w2", 2 * P, ST))
+        o = ("psB", 0, NB)
+        mm(o, ("ident",), ("c2b", 0, 768, 2), True, False)
+        mm(o, ("ident",), ("c2b", 1, 768, 2), False, False)
+        mm(o, ("ident",), ("w1", 2 * P, ST, 2), False, False)
+        mm(o, ("ident",), ("w1", 2 * P + 1, ST, 2), False, True)
+        tc("v", ("fsend",), o)
+        send("f%d" % s, "fsend", "L%d" % s, 0, -1)
+
+    def own_flags(s):
+        a = 2 * BS * s
+        tc("s", ("c2w",), ("w2", a, a + 1024))
+        for r in range(16):
+            for b in range(2):
+                mm(("psA", 0, 32), cmat(r), ("w1", a + 2 * r + b, a + 1024, 32), r + b == 0, False)
+        for r in range(16):
+            for b in range(2):
+                mm(("psA", 0, 32), cmat(r), ("c2w", 2 * r + b, 1024, 32), False, False)
+
+    def their_flags(s):
+        k = 32 * (s - 1)
+        w = ("L%d" % (s - 1),)
+        gat("s", ("Lg", 256, 512), w, ("binv", k + 16, k + 32))
+        gat("v", ("Lg", 0, 256), w, ("binv", k, k + 16))
+        for r in range(16):
+            mm(("psA", 0, 32), cmat(r), ("Lg", r, 512, 16), False, r == 15)
+
+    def bwd(s, W, O, hook):
+        def scan(c):
+            i, o = ("cb", 1024 * c, 1024 * c + 1024), ("scn%d" % (c % 2),)
+            op("v", lambda: g.vector.tensor_tensor_scan(ap(o), ap(("d0",)), ap(i), 191.0, OP.max, OP.min), [i, ("d0",)], [o])
+            r = (64 * c, 64 * c + 64)
+            tt(("ai",) + r, ("scn%d" % (c % 2), 15, 1024, 16), ("xm%d" % s,) + r, OP.add)
+
+        def dead(k):
+            r = (128 * k, 128 * k + 128)
+            ts(("d255",) + r, ("psA",) + r, 1.5, OP.is_ge, 255.0, OP.mult)
+            tt((W,) + r, ("hi",) + r, ("d255",) + r, OP.max)
+
+        def post(c, cn):
+            ts(("mt", 64 * c, 64 * c + 64), cn, 8.5, OP.is_ge)
+            if c % 2:
+                r = (64 * c - 64, 64 * c + 64)
+                mm(("psA",) + r, ("B",), ("mt",) + r, True, True)
+
+        def halves():
+            ts(("hi",), ("ai",), 1, OP.arith_shift_right)
+            dead(0)
+
+        def h3():
+            scan(1)
+            if hook:
+                hook()
+        match(s, W, YO, "cb", 32, post,
+              {"g2": lambda: scan(0), "g3": h3, "p0": lambda: scan(2), "p1": lambda: scan(3), "l3": halves}, False)
+        dead(1)
+        a = YO + BS * s
+        gat("s", (O, a + 256, a + 512), (W, 0, YO + P), ("sb16_%d" % s, 16, 32))
+        gat("v", (O, a, a + 256), (W, 0, YO + P), ("sb16_%d" % s, 0, 16))
+
+    def border_y(name, Y):
+        win = (Y, YO, YO + P)
+        gat("s", ("ysend", 192, 384), win, ("snd16", 12, 24))
+        gat("v", ("ysend", 0, 192), win, ("snd16", 0, 12))
+        return send(name, "ysend", Y, YO + P, 1)
+
+    for r in range(16):
+        mm(("psA", 0, 32), cmat(r), ("sdrep", r, BS, 16), r == 0, r == 15)
+    pack(0)
+    lists(0)
+    slots(0)
+    fill(("cst",), 30.0)
+    fill(("bw",), float(NB // 2))
+    sca(("bw",), ("snd16",), ("io384",))
+    for r in range(16):
+        mm(("psB", 0, 64), cmat(r), ("bw", BS + r, 3 * BS, 16), r == 0, r == 15)
+    ts(("binv",), ("psB", 0, 64), 1.0 / 16, OP.mult, float(NB // 2), OP.add)
+    fill(("L0", NB, 400), 0.0)
+    fill(("L1", NB, 400), 0.0)
+    need("y", [("rs_x", total["rs_x"])])
+    dma("y", "ya", [(T.ya[:, YO:YO + P], T.y0[:, :])], [], [("ya", YO, YO + P)])
+    dma("y", "yb", [(T.yb[:, YO:YO + P], T.y0[:, :])], [], [("yb", YO, YO + P)])
+
+    fwd_match(0, {}, True)
+    flags_out(0)
+    own_flags(1)
+    pack(1)
+    fill(("comp", 0, CAP), 255)
+    fill(("d0",), 0.0)
+    fill(("d0", 0, 1024, 16), 191.0)
+    gat("s", ("ysend",), ("ya", YO, YO + P), ("snd16",))
+    their_flags(1)
+    need("g", [("rs_f0", total["rs_f0"])])
+    send("y", "ysend", "ya", YO + P, 1)
+    lists(1)
+    fwd_match(1, {"g2": lambda: slots(1)}, True)
+    flags_out(1)
+    own_flags(2)
+    pack(2)
+    fill(("comp", 0, CAP), 255)
+    fill(("mw", 0, CAP), 1.0)
+    fill(("mw", CAP, CAP + 1536), 0.0)
+    fill(("memblk",), 0.0)
+    ts(("snd2i",), ("snd32",), 2, OP.mult)
+    tc("v", ("snd2",), ("snd2i",))
+    members(0)
+    members(1)
+    their_flags(2)
+    lists(2)
+    take_xt(2)
+    slots(2)
+    bwd(2, "ya", "yb", None)
+    border_y("b2", "yb")
+    dma("y", "cy", [(T.ya[:, YO + 2 * BS:YO + 3 * BS], T.yb[:, YO + 2 * BS:YO + 3 * BS])],
+        [("yb", YO + 2 * BS, YO + 3 * BS)], [("ya", YO + 2 * BS, YO + 3 * BS)])
+    dma("y", "o2", [(T.yv[:, 2 * BS:3 * BS], T.yb[:, YO + 2 * BS:YO + 3 * BS])], [("yb", YO + 2 * BS, YO + 3 * BS)], [])
+    fwd_match(2, {}, False)
+    members(2)
+    dma("y", "blm", [(T.memblk[b::16, 0:min(336, 1536 - 336 * b)], T.memrep[b::16, 336 * b:min(1536, 336 * b + 336)]) for b in range(5)],
+        [("memrep",)], [("memblk",)])
+    bwd(1, "yb", "ya", None)
+    border_y("b1", "ya")
+    dma("y", "o1", [(T.yv[:, BS:2 * BS], T.ya[:, YO + BS:YO + 2 * BS])], [("ya", YO + BS, YO + 2 * BS)], [])
+    flags_out(2)
+    dma("y", "bl2", [(T.w2blk[b::16, :], T.w2[b::16, 672 * b:672 * b + 672]) for b in range(16)], [("w2", 0, 2 * P)], [("w2blk",)])
+
+    def last_flags():
+        w, o, i = ("w1", 0, 2 * P), ("tmpR",), ("L2", 0, NB)
+        op("v", lambda: g.vector.tensor_tensor(ap(o), ap(w).indirect(ap(("snd2",))), ap(i), OP.add), [w, i, ("snd2",)], [o])
+        sca(w, ("snd2",), o)
+        dma("y", "bl1", [(T.w1blk[b::16, :], T.w1[b::16, 672 * b:672 * b + 672]) for b in range(16)], [w], [("w1blk",)])
+    bwd(0, "ya", "yb", last_flags)
+    dma("y", "o0", [(T.yv[:, 0:BS], T.yb[:, YO:YO + BS])], [("yb", YO, YO + BS)], [])
+    tc("s", ("w2bb",), ("w2blk",))
+    parts = [("sdblk",), ("w1blk", 0, 672, 2), ("w1blk", 1, 672, 2), ("w2bb", 0, 672, 2), ("w2bb", 1, 672, 2)]
+    for k, r in enumerate(parts):
+        mm(("psB", 0, 336), ("ident",), r, k == 0, k == len(parts) - 1)
+    ts(("yfl",), ("psB", 0, 336), 0.25, OP.is_gt)
+    tt(("yfb",), ("yfl",), ("memblk",), OP.add)
+    dma("s", "of", [(T.yf[:, :], T.yfb[:, :])], [("yfb",)], [])
+    need("g", [(s, n) for s, n in total.items()])
+    for s, n in total.items():
+        if s != "qg" and known["g"].get(s, 0) < n:
+            g.wait_ge(T.sem[s], n)

@@ -4,8 +4,23 @@ from concourse.mybir import AluOpType as OP, ActivationFunctionType as AF
 P, PL, NB, BS, CAP, BK = 5376, 5760, 384, 512, 256, 128
 ST = 2 * PL
 WW = ST + 1024
+ZV, ZS = 6144, 9216
 BIG = 1023.0
 YO = CAP
+SPLITF, SPLITB = (40, 40, 40, 40), (30, 30, 34, 44)
+
+BT = " G2 X1 N0 L0 A1 G3 N1 C0 X2 L1 A2 P0 N2 C1 X3 L2 A3 "
+BE = " P1 B0 N3 C2 H L3 D0 P2 C3 P3 B1 D1 U "
+FT = " G0 T c G1 X0 A0 G2 X1 L0 A1 G3 C0 X2 L1 A2 P0 C1 X3 L2 A3 P1 C2 S0-4 S4-8 P2 V8-10 L3 C3 V10-12 P3 V12-16 F"
+SCHED = {
+    "out0": "f0" + FT,
+    "out1": "f1" + FT,
+    "back2": "b2 G0 T c G1 X0 A0" + BT + "; f2 g0 g1 ; b2" + BE + "Y",
+    "gap1": "f2 Q v0 v1 X0 A0 G2 X1 L0 A1 G3 C0 X2 L1 A2 P0 C1 X3 ; b1 g0 ; f2 L2 A3 P1 C2 ; b1 v0 g1 ; f2 L3 P2 C3 ; b1 v1 ; f2 P3",
+    "back1": "b1 X0 A0" + BT + "; f2 S0-2 ; b1" + BE + "Y",
+    "gap0": "f2 S2-6 S6-8 V8-12 V12-16 F M",
+    "back0": "b0 G0 G1 X0 A0" + BT + "W R" + BE,
+}
 
 SCRATCH = {
     "xw": ("sbuf", [128, PL], "bfloat16"),
@@ -15,13 +30,14 @@ SCRATCH = {
     "snd2i": ("sbuf", [128, 24], "int32"),
     "ci": ("sbuf", [128, 256], "int32"), "xi": ("sbuf", [128, 256], "int32"), "vt": ("sbuf", [128, 256], "int32"),
     "cf": ("sbuf", [128, 4096], "bfloat16"), "cb": ("sbuf", [128, 4096], "bfloat16"),
-    "d0": ("sbuf", [128, 1024], "bfloat16"), "mt": ("sbuf", [128, 256], "bfloat16"),
-    "ai": ("sbuf", [128, 256], "int32"), "hi": ("sbuf", [128, 256], "int32"), "d255": ("sbuf", [128, 256], "float32"),
-    "nm": ("sbuf", [128, 256], "float32"), "vo": ("sbuf", [128, 256], "uint16"), "trash": ("sbuf", [128, 64], "float32"),
+    "scn": ("sbuf", [128, 4096], "bfloat16"),
+    "d0": ("sbuf", [128, 1024], "bfloat16"), "mt": ("sbuf", [128, 256], "bfloat16"), "hi": ("sbuf", [128, 256], "int32"),
+    "vo": ("sbuf", [128, 256], "uint16"), "trash": ("sbuf", [128, 64], "float32"),
     "w1": ("sbuf", [128, WW], "bfloat16"), "w2": ("sbuf", [128, WW], "float32"),
     "ones": ("sbuf", [128, 1024], "bfloat16"), "cst": ("sbuf", [128, 1024], "float32"),
-    "C": ("sbuf", [128, 2048], "bfloat16"), "R": ("sbuf", [128, 2048], "bfloat16"),
+    "C": ("sbuf", [128, 2048], "bfloat16"), "R": ("sbuf", [128, 2048], "bfloat16"), "neg": ("sbuf", [128, 128], "bfloat16"),
     "ident": ("sbuf", [128, 128], "bfloat16"), "B": ("sbuf", [128, 128], "bfloat16"), "A1": ("sbuf", [128, 128], "bfloat16"),
+    "hI": ("sbuf", [128, 128], "bfloat16"), "qI": ("sbuf", [128, 128], "bfloat16"),
     "sdrep": ("sbuf", [128, 512], "bfloat16"), "sdblk": ("sbuf", [128, 336], "bfloat16"),
     "L0": ("sbuf", [128, 400], "bfloat16"), "L1": ("sbuf", [128, 400], "bfloat16"), "L2": ("sbuf", [128, 400], "bfloat16"),
     "Lg": ("sbuf", [128, 512], "bfloat16"), "fsend": ("sbuf", [128, NB], "bfloat16"),
@@ -36,7 +52,7 @@ SCRATCH = {
     "mw": ("sbuf", [128, CAP + 1536], "bfloat16"), "memrep": ("sbuf", [128, 1536], "bfloat16"),
     "memblk": ("sbuf", [128, 336], "bfloat16"), "w1blk": ("sbuf", [128, 672], "bfloat16"),
     "w2blk": ("sbuf", [128, 672], "float32"), "w2bb": ("sbuf", [128, 672], "bfloat16"),
-    "tmpR": ("sbuf", [128, NB], "bfloat16"), "yfl": ("sbuf", [128, 336], "float32"), "yfb": ("sbuf", [128, 336], "bfloat16"),
+    "tmpR": ("sbuf", [128, NB], "bfloat16"), "yfb": ("sbuf", [128, 336], "bfloat16"),
     "psd0": ("psum", [128, 1024], "float32"), "psd1": ("psum", [128, 1024], "float32"),
     "cnt0": ("psum", [128, 512], "float32"), "cnt1": ("psum", [128, 512], "float32"),
     "psA": ("psum", [128, 512], "float32"), "psB": ("psum", [128, 512], "float32"),
@@ -49,11 +65,10 @@ for _s in range(3):
     SCRATCH["vs%d" % _s] = ("sbuf", [128, 32], "float32")
     SCRATCH["ab%d" % _s] = ("sbuf", [128, 1024], "bfloat16")
     SCRATCH["nr%d" % _s] = ("sbuf", [128, 1024], "bfloat16")
-for _s in range(2):
-    SCRATCH["scn%d" % _s] = ("sbuf", [128, 1024], "bfloat16")
 
 _EX = ["x", "f0", "y", "f1", "b2", "f2", "b1"]
-_DM = ["snd", "xa", "xb", "tl", "sd", "cd0", "cd1", "sk", "ya", "yb", "bl1", "bl2", "blm", "cy", "o2", "o1", "o0", "of"]
+_DM = ["snd", "xa", "xb", "tl", "sd", "cd0", "cd1", "sk", "zz", "zv", "ya", "yb", "bl1", "bl2", "blm", "cy", "o2", "o1",
+       "o0", "of"]
 SEMAPHORES = ["qv", "qs", "qt", "qg"] + ["ls_" + e for e in _EX] + ["rs_" + e for e in _EX] + ["d_" + d for d in _DM]
 
 
@@ -114,10 +129,9 @@ def rank_program(g, core, T, topo):
             n, a, b = reg(r)
             if is_ps(n):
                 a, b = 0, width(n)
-            if len(r) <= 3 and not is_ps(n):
-                recs[n] = [e for e in recs.get(n, []) if not (a <= e[0] and e[1] <= b)]
-            elif is_ps(n):
                 recs[n] = [e for e in recs.get(n, []) if q == "t" and e[3] == "t"]
+            elif len(r) <= 3:
+                recs[n] = [e for e in recs.get(n, []) if not (a <= e[0] and e[1] <= b)]
             recs.setdefault(n, []).append((a, b, True, q, ev))
         for r in R:
             n, a, b = reg(r)
@@ -145,11 +159,14 @@ def rank_program(g, core, T, topo):
             eng[q].dma_start(o, i).then_inc(T.sem["d_" + name], 16)
         note(q, R, W, event(q, "d_" + name, 16 * len(pairs)))
 
+    def act(o, i, f, **k):
+        op("s", lambda: g.scalar.activation(ap(o), ap(i), f, **k), [i], [o])
+
     def tc(q, o, i):
         if q == "v":
             op("v", lambda: g.vector.tensor_copy(ap(o), ap(i)), [i], [o])
         else:
-            op("s", lambda: g.scalar.activation(ap(o), ap(i), AF.Copy), [i], [o])
+            act(o, i, AF.Copy)
 
     def gat(q, o, win, off):
         if q == "v":
@@ -174,6 +191,10 @@ def rank_program(g, core, T, topo):
 
     def mm(o, l, r, start, stop):
         op("t", lambda: g.tensor.matmul(ap(o), ap(l), ap(r), start, stop), [l, r], [o])
+
+    def sums(o, terms):
+        for k, (l, r) in enumerate(terms):
+            mm(o, l, r, k == 0, k == len(terms) - 1)
 
     def sel(o, i, pattern, cmp, fl, base, cm):
         op("g", lambda: g.affine_select(ap(o), ap(i), pattern, cmp, fl, base, cm), [i], [o])
@@ -208,66 +229,20 @@ def rank_program(g, core, T, topo):
         total["rs_" + name] = cnt
         ev = ("rs_" + name, cnt)
         clock[ev] = {"rs_" + name: cnt}
-        recs.setdefault(dst, [])
-        recs[dst] = [e for e in recs[dst] if not (col <= e[0] and e[1] <= col + NB)]
+        recs[dst] = [e for e in recs.get(dst, []) if not (col <= e[0] and e[1] <= col + NB)]
         recs[dst].append((col, col + NB, True, "r", ev))
-        return ev
 
     def cmat(r):
         return ("C", 128 * r, 128 * r + 128)
-
-    h = P // 2
-    dma("y", "snd", [(T.snd32[:, :], T.snd[:, :])], [], [("snd32",)])
-    dma("y", "xa", [(T.xw[:, 0:h], T.x[:, 0:h])], [], [("xw", 0, h)])
-    dma("s", "xb", [(T.xw[:, h:P], T.x[:, h:P])], [], [("xw", h, P)])
-    fill(("sdrep",), 0.0)
-    fill(("ones",), 1.0)
-    fill(("R",), -1.0)
-    fill(("sdblk",), 0.0)
-    fill(("C",), 0.0)
-    dma("y", "sd", [(T.sdrep[0::16, :], T.sd[:, :])], [], [("sdrep",)])
-    dma("y", "cd0", [(T.cdt[:, 0:BS], T.cd[:, 0:BS])], [], [("cdt", 0, BS)])
-    dma("y", "tl", [(T.tlb[:, :], T.tl[:, :])], [], [("tlb",)])
-    dma("y", "sk", [(T.sdblk[0::16, :], T.sd[:, 0:336]), (T.sdblk[1::16, 0:BS - 336], T.sd[:, 336:BS])], [], [("sdblk",)])
-    dma("y", "cd1", [(T.cdt[:, BS:3 * BS], T.cd[:, BS:3 * BS])], [], [("cdt", BS, 3 * BS)])
-
-    sel(("B",), ("ones", 0, 128), [[-16, 8], [0, 16]], OP.is_ge, 0.0, 0, 1)
-    sel(("B",), ("B",), [[16, 8], [0, 16]], OP.is_ge, 0.0, 15, -1)
-    sel(("A1",), ("R", 0, 128), [[16, 8], [0, 16]], OP.is_ge, 0.0, 15, -1)
-    sel(("A1",), ("A1",), [[-1, 128]], OP.is_gt, 0.0, 0, 1)
-    sel(("A1",), ("A1",), [[-1, 128]], OP.not_equal, -(BIG + 1), 0, 1)
-    iota(("itp",), [[0, 64]], 0, 1)
-    iota(("it3",), [[16, 32]], BS, 0)
-    iota(("it2",), [[16, 64]], ST, 0)
-    sel(("ident",), ("ones", 0, 128), [[-1, 128]], OP.is_equal, 0.0, 0, 1)
-
-    op("s", lambda: g.scalar.activation(ap(("warm",)), ap(("ones", 0, 8)), AF.Sigmoid), [("ones", 0, 8)], [("warm",)])
-    for a in range(0, ST, 1024):
-        b = min(ST, a + 1024)
-        op("s", lambda a=a, b=b: g.scalar.activation(ap(("w2", a, b)), ap(("ones", 0, b - a)), AF.Copy, scale=0.0),
-           [("ones", 0, b - a)], [("w2", a, b)])
-
-    for q in range(8):
-        tc("v", ("C", 16 * q, 16 * q + 129 * 15 + 1, 129), ("B", 16 * q, 16 * q + 16))
-    tc("v", ("snd16",), ("snd32",))
-    fill(("one32",), 1.0)
-    ts(("itp",), ("itp",), 15, OP.bitwise_and)
-    tt(("t512",), ("it3",), ("itp", 0, 32), OP.add)
-    tt(("trash",), ("it2",), ("itp",), OP.add)
-    for s in range(3):
-        ts(("vs%d" % s,), ("t512",), float(512 * s - 256), OP.add)
-    fill(("w1", 0, ST), 0.0)
-    fill(("comp", 0, CAP), 255)
-
-    gat("v", ("xsend",), ("xw", 0, P), ("snd16",))
-    send("x", "xsend", "xw", P, 1)
-    sel(("R",), ("R",), [[-1, 128], [0, 16]], OP.is_equal, 0.0, 0, 1)
-    iota(("io384",), [[1, NB]], -NB // 2, 0)
 
     def pack(s):
         r = ("cdt", BS * s, BS * s + BS)
         ts(r, r, 256, OP.mult)
         tt(r, r, ("xw", BS * s, BS * s + BS), OP.add)
+
+    def offsets(s, a, b):
+        ts(("ci", a, b), ("comp", a, b), 9, OP.arith_shift_right)
+        tc("v", ("c16_%d" % s, a, b), ("ci", a, b))
 
     def lists(s):
         ts(("flw",), ("psA", 0, 32), 0.25, OP.is_gt)
@@ -279,35 +254,51 @@ def rank_program(g, core, T, topo):
         tt(("sl",), ("pp",), ("t512",), OP.min)
         tc("v", ("sl16",), ("sl",))
         sca(("comp",), ("sl16",), ("cdt", BS * s, BS * s + BS))
-        m = ("comp", 0, CAP)
-        ts(("ci",), m, 9, OP.arith_shift_right)
-        tc("v", ("c16_%d" % s,), ("ci",))
-        ts(("xi",), m, 255, OP.bitwise_and)
+        offsets(s, 0, 128)
+        ts(("xi",), ("comp", 0, CAP), 255, OP.bitwise_and)
         tc("v", ("xm%d" % s,), ("xi",))
         for k in range(2):
             mm(("psA", 128 * k, 128 * k + 128), ("xm%d" % s, 128 * k, 128 * k + 128), ("ident",), True, True)
 
-    def take_xt(s):
-        tc("s", ("xT%d" % s,), ("psA", 0, 256))
-
     def slots(s):
-        ts(("vt",), ("comp", 0, CAP), 8, OP.arith_shift_right)
         ts(("zz",), ("pp",), 255.5, OP.is_gt, 8192.0, OP.mult)
         tt(("zz",), ("pp",), ("zz",), OP.add)
         tt(("zz",), ("zz",), ("vs%d" % s,), OP.min)
         tc("v", ("sb16_%d" % s,), ("zz",))
 
-    def members(s):
-        gat("s", ("memrep", BS * s, BS * s + BS), ("mw",), ("sb16_%d" % s,))
+    def own_flags(s):
+        a = 2 * BS * s
+        tc("s", ("c2w",), ("w2", a, a + 1024))
+        for n, lo, hi in (("w1", a, a + 1024), ("c2w", 0, 1024)):
+            for r in range(16):
+                for b in range(2):
+                    mm(("psA", 0, 32), cmat(r), (n, lo + 2 * r + b, hi, 32), n == "w1" and r + b == 0, False)
 
-    def match(s, wn, w0, cand, split, post, hook, fresh):
-        win = (wn, w0, w0 + PL)
-        off = "c16_%d" % s
+    def their_flags(s):
+        k = 32 * (s - 1)
+        w = ("L%d" % (s - 1),)
+        gat("s", ("Lg", 256, 512), w, ("binv", k + 16, k + 32))
+        gat("v", ("Lg", 0, 256), w, ("binv", k, k + 16))
+        for r in range(16):
+            mm(("psA", 0, 32), cmat(r), ("Lg", r, 512, 16), False, r == 15)
+
+    def stream(name):
+        s, out = int(name[1]), name[0] == "f"
+        wn, w0, cand, split = ("xw", 0, "cf", SPLITF) if out else (("ya", "yb")[s % 2], YO, "cb", SPLITB)
+        ot = ("yb", "ya")[s % 2]
+        win, off = (wn, w0, w0 + PL), "c16_%d" % s
+
+        def gs(c):
+            k, j, n = 64 * c, 1024 * c, split[c]
+            gat("s", (cand, j + 16 * n, j + 1024), win, (off, k + n, k + 64))
+
+        def gv(c):
+            k, j, n = 64 * c, 1024 * c, split[c]
+            gat("v", (cand, j, j + 16 * n), win, (off, k, k + n))
 
         def G(c):
-            k, j = 64 * c, 1024 * c
-            gat("s", (cand, j + 16 * split, j + 1024), win, (off, k + split, k + 64))
-            gat("v", (cand, j, j + 16 * split), win, (off, k, k + split))
+            gs(c)
+            gv(c)
 
         def X(c):
             ps, hf = "psd%d" % (c % 2), c // 2
@@ -318,193 +309,219 @@ def rank_program(g, core, T, topo):
                 j = 1024 * c + 512 * b
                 mm((ps, 512 * b, 512 * b + 512), ("ident",), (cand, j, j + 512), False, True)
 
-        def Ab(c):
-            o, i = ("ab%d" % (c % 3),), ("psd%d" % (c % 2),)
-            op("s", lambda: g.scalar.activation(ap(o), ap(i), AF.Abs), [i], [o])
+        def A(c):
+            act(("ab%d" % (c % 3),), ("psd%d" % (c % 2),), AF.Abs)
 
-        def Le(c):
+        def L(c):
             o, i = ("nr%d" % (c % 3),), ("ab%d" % (c % 3),)
             op("v", lambda: g.vector.tensor_scalar(ap(o), ap(i), ap(("tlb",)), None, OP.is_le), [i, ("tlb",)], [o])
 
-        def Ct(c):
-            k = 64 * (c // 2)
-            for i in range(16):
-                mm(("cnt%d" % (c % 2), k, k + 64), cmat(i), ("nr%d" % (c % 3), i, 1024, 16), i == 0, i == 15)
+        def cn(c, at=0):
+            k = at + 64 * (c // 2)
+            return ("cnt%d" % (c % 2), k, k + 64)
 
-        def Po(c):
-            k = 64 * (c // 2)
-            post(c, ("cnt%d" % (c % 2), k, k + 64))
+        def C(c):
+            sums(cn(c), [(cmat(i), ("nr%d" % (c % 3), i, 1024, 16)) for i in range(16)])
 
-        def hk(n):
-            if n in hook:
-                hook[n]()
-
-        G(0)
-        if fresh:
-            take_xt(s)
-        G(1); X(0); Ab(0); G(2); hk("g2"); X(1); Le(0); Ab(1); G(3); hk("g3"); Ct(0); X(2); Le(1); Ab(2); Po(0); hk("p0")
-        Ct(1); X(3); Le(2); Ab(3); Po(1); hk("p1"); Ct(2); Le(3); hk("l3"); Po(2); Ct(3); Po(3)
-
-    def fwd_match(s, hook, fresh):
-        def post(c, cn):
+        def Pt(c):
             r = (64 * c, 64 * c + 64)
-            nm = ("nm",) + r
-            ts(nm, cn, 8.5, OP.is_lt, 30000.0, OP.mult)
-            tt(nm, nm, ("trash",), OP.min)
-            tt(nm, nm, ("vt",) + r, OP.max)
-            tc("v", ("vo",) + r, nm)
-        match(s, "xw", 0, "cf", 40, post, hook, fresh)
+            if out:
+                m = cn(c, 256)
+                ts(m, cn(c), 8.5, OP.is_lt, 30000.0, OP.mult)
+                tt(m, m, ("trash",), OP.min)
+                tt(m, m, ("vt",) + r, OP.max)
+                tc("v", ("vo",) + r, m)
+            else:
+                ts(("mt",) + r, cn(c), 8.5, OP.is_ge)
 
-    def scatter_s(c):
-        w, o = ("w2",), ("vo", 64 * c, 64 * c + 64)
-        op("s", lambda: g.scalar.activation(ap(w).indirect(ap(o)), ap(("cst",)), AF.Sigmoid), [o, ("cst",)], [w])
+        def S(a, b):
+            w, o, i = ("w2",), ("vo", 16 * a, 16 * b), ("cst", 0, 256 * (b - a))
+            op("s", lambda: g.scalar.activation(ap(w).indirect(ap(o)), ap(i), AF.Sigmoid), [o, i], [w])
 
-    def scatter_v(c):
-        sca(("w1",), ("vo", 64 * c, 64 * c + 64), ("ones",))
+        def V(a, b):
+            sca(("w1",), ("vo", 16 * a, 16 * b), ("ones", 0, 256 * (b - a)))
 
-    def flags_out(s):
-        scatter_s(0); scatter_s(1); scatter_v(2); scatter_v(3)
-        tc("s", ("c2b",), ("w2", 2 * P, ST))
-        o = ("psB", 0, NB)
-        mm(o, ("ident",), ("c2b", 0, 768, 2), True, False)
-        mm(o, ("ident",), ("c2b", 1, 768, 2), False, False)
-        mm(o, ("ident",), ("w1", 2 * P, ST, 2), False, False)
-        mm(o, ("ident",), ("w1", 2 * P + 1, ST, 2), False, True)
-        tc("v", ("fsend",), o)
-        send("f%d" % s, "fsend", "L%d" % s, 0, -1)
+        def F():
+            tc("s", ("c2b",), ("w2", 2 * P, ST))
+            i = ("ident",)
+            sums(("psB", 0, NB), [(i, ("c2b", 0, 768, 2)), (i, ("c2b", 1, 768, 2)), (i, ("w1", 2 * P, ST, 2)), (i, ("w1", 2 * P + 1, ST, 2))])
+            tc("v", ("fsend",), ("psB", 0, NB))
+            send("f%d" % s, "fsend", "L%d" % s, 0, -1)
 
-    def own_flags(s):
-        a = 2 * BS * s
-        tc("s", ("c2w",), ("w2", a, a + 1024))
-        for r in range(16):
-            for b in range(2):
-                mm(("psA", 0, 32), cmat(r), ("w1", a + 2 * r + b, a + 1024, 32), r + b == 0, False)
-        for r in range(16):
-            for b in range(2):
-                mm(("psA", 0, 32), cmat(r), ("c2w", 2 * r + b, 1024, 32), False, False)
-
-    def their_flags(s):
-        k = 32 * (s - 1)
-        w = ("L%d" % (s - 1),)
-        gat("s", ("Lg", 256, 512), w, ("binv", k + 16, k + 32))
-        gat("v", ("Lg", 0, 256), w, ("binv", k, k + 16))
-        for r in range(16):
-            mm(("psA", 0, 32), cmat(r), ("Lg", r, 512, 16), False, r == 15)
-
-    def bwd(s, W, O, hook):
-        def scan(c):
-            i, o = ("cb", 1024 * c, 1024 * c + 1024), ("scn%d" % (c % 2),)
+        def N(c):
+            i, o = ("cb", 1024 * c, 1024 * c + 1024), ("scn", 1024 * c, 1024 * c + 1024)
             op("v", lambda: g.vector.tensor_tensor_scan(ap(o), ap(("d0",)), ap(i), 191.0, OP.max, OP.min), [i, ("d0",)], [o])
-            r = (64 * c, 64 * c + 64)
-            tt(("ai",) + r, ("scn%d" % (c % 2), 15, 1024, 16), ("xm%d" % s,) + r, OP.add)
 
-        def dead(k):
+        def H():
+            sums(("psB", 0, 256), [(("hI",), ("xm%d" % s,)), (("qI",), ("ones", 0, 256)), (("hI",), ("scn", 15, 4096, 16))])
+            tc("v", ("hi",), ("psB", 0, 256))
+
+        def Bm(k):
+            mm(("psA", 128 * k, 128 * k + 128), ("B",), ("mt", 128 * k, 128 * k + 128), True, True)
+
+        def D(k):
             r = (128 * k, 128 * k + 128)
-            ts(("d255",) + r, ("psA",) + r, 1.5, OP.is_ge, 255.0, OP.mult)
-            tt((W,) + r, ("hi",) + r, ("d255",) + r, OP.max)
+            m = ("psA", 256 + 128 * k, 384 + 128 * k)
+            ts(m, ("psA",) + r, 1.5, OP.is_ge, 255.0, OP.mult)
+            tt((wn,) + r, ("hi",) + r, m, OP.max)
 
-        def post(c, cn):
-            ts(("mt", 64 * c, 64 * c + 64), cn, 8.5, OP.is_ge)
-            if c % 2:
-                r = (64 * c - 64, 64 * c + 64)
-                mm(("psA",) + r, ("B",), ("mt",) + r, True, True)
+        def U():
+            a = YO + BS * s
+            gat("s", (ot, a + 256, a + 512), (wn, 0, YO + P), ("sb16_%d" % s, 16, 32))
+            gat("v", (ot, a, a + 256), (wn, 0, YO + P), ("sb16_%d" % s, 0, 16))
 
-        def halves():
-            ts(("hi",), ("ai",), 1, OP.arith_shift_right)
-            dead(0)
+        def Y():
+            w = (ot, YO, YO + P)
+            gat("s", ("ysend", 192, 384), w, ("snd16", 12, 24))
+            gat("v", ("ysend", 0, 192), w, ("snd16", 0, 12))
+            send("b%d" % s, "ysend", ot, YO + P, 1)
+            r = (YO + BS * s, YO + BS * s + BS)
+            dma("y", "o%d" % s, [(T.yv[:, BS * s:BS * s + BS], ap((ot,) + r))], [(ot,) + r], [])
+            if s == 2:
+                dma("y", "cy", [(ap((wn,) + r), ap((ot,) + r))], [(ot,) + r], [(wn,) + r])
 
-        def h3():
-            scan(1)
-            if hook:
-                hook()
-        match(s, W, YO, "cb", 32, post,
-              {"g2": lambda: scan(0), "g3": h3, "p0": lambda: scan(2), "p1": lambda: scan(3), "l3": halves}, False)
-        dead(1)
-        a = YO + BS * s
-        gat("s", (O, a + 256, a + 512), (W, 0, YO + P), ("sb16_%d" % s, 16, 32))
-        gat("v", (O, a, a + 256), (W, 0, YO + P), ("sb16_%d" % s, 0, 16))
+        def Tk():
+            tc("s", ("xT%d" % s,), ("psA", 0, 256))
 
-    def border_y(name, Y):
-        win = (Y, YO, YO + P)
-        gat("s", ("ysend", 192, 384), win, ("snd16", 12, 24))
-        gat("v", ("ysend", 0, 192), win, ("snd16", 0, 12))
-        return send(name, "ysend", Y, YO + P, 1)
+        def ck():
+            offsets(s, 128, 256)
 
-    for r in range(16):
-        mm(("psA", 0, 32), cmat(r), ("sdrep", r, BS, 16), r == 0, r == 15)
+        def Q():
+            ts(("vt",), ("comp", 0, CAP), 8, OP.arith_shift_right)
+
+        def R():
+            w, o, i = ("w1", 0, 2 * P), ("tmpR",), ("L2", 0, NB)
+            op("v", lambda: g.vector.tensor_tensor(ap(o), ap(w).indirect(ap(("snd2",))), ap(i), OP.add), [w, i, ("snd2",)], [o])
+            sca(w, ("snd2",), o)
+            dma("y", "bl1", [(T.w1blk[b::16, :], T.w1[b::16, 672 * b:672 * b + 672]) for b in range(16)], [w], [("w1blk",)])
+
+        def M():
+            gat("s", ("memrep", BS * s, BS * s + BS), ("mw",), ("sb16_%d" % s,))
+            if s == 2:
+                dma("y", "bl2", [(T.w2blk[b::16, :], T.w2[b::16, 672 * b:672 * b + 672]) for b in range(16)], [("w2", 0, 2 * P)], [("w2blk",)])
+                dma("y", "blm", [(T.memblk[b::16, 0:min(336, 1536 - 336 * b)], T.memrep[b::16, 336 * b:min(1536, 336 * b + 336)])
+                                 for b in range(5)], [("memrep",)], [("memblk",)])
+
+        def W():
+            tc("s", ("w2bb",), ("w2blk",))
+        return {"G": G, "g": gs, "v": gv, "X": X, "A": A, "L": L, "C": C, "P": Pt, "S": S, "V": V, "F": F, "N": N, "H": H,
+                "B": Bm, "D": D, "U": U, "Y": Y, "T": Tk, "c": ck, "Q": Q, "R": R, "M": M, "W": W}
+
+    streams = {n: stream(n) for n in ("f0", "f1", "f2", "b2", "b1", "b0")}
+
+    def play(key):
+        for part in SCHED[key].split(";"):
+            words = part.split()
+            for w in words[1:]:
+                streams[words[0]][w[0]](*[int(a) for a in w[1:].split("-") if a])
+
+    h = P // 2
+    dma("y", "xa", [(T.xw[:, 0:h], T.x[:, 0:h])], [], [("xw", 0, h)])
+    dma("s", "snd", [(T.snd32[:, :], T.snd[:, :])], [], [("snd32",)])
+    dma("s", "xb", [(T.xw[:, h:P], T.x[:, h:P])], [], [("xw", h, P)])
+    fill(("sdrep",), 0.0)
+    fill(("ones",), 1.0)
+    fill(("neg",), -1.0)
+    fill(("sdblk",), 0.0)
+    dma("y", "sd", [(T.sdrep[0::16, :], T.sd[:, :])], [], [("sdrep",)])
+    dma("y", "cd0", [(T.cdt[:, 0:BS], T.cd[:, 0:BS])], [], [("cdt", 0, BS)])
+    dma("y", "tl", [(T.tlb[:, :], T.tl[:, :])], [], [("tlb",)])
+    dma("y", "sk", [(T.sdblk[0::16, :], T.sd[:, 0:336]), (T.sdblk[1::16, 0:BS - 336], T.sd[:, 336:BS])], [], [("sdblk",)])
+    dma("y", "cd1", [(T.cdt[:, BS:3 * BS], T.cd[:, BS:3 * BS])], [], [("cdt", BS, 3 * BS)])
+
+    sel(("B",), ("ones", 0, 128), [[-16, 8], [0, 16]], OP.is_ge, 0.0, 0, 1)
+    sel(("B",), ("B",), [[16, 8], [0, 16]], OP.is_ge, 0.0, 15, -1)
+    iota(("itp",), [[0, 64]], 0, 1)
+    iota(("it3",), [[16, 32]], BS, 0)
+    sel(("A1",), ("neg",), [[16, 8], [0, 16]], OP.is_ge, 0.0, 15, -1)
+    sel(("A1",), ("A1",), [[-1, 128]], OP.is_gt, 0.0, 0, 1)
+    sel(("A1",), ("A1",), [[-1, 128]], OP.not_equal, -(BIG + 1), 0, 1)
+    sel(("ident",), ("ones", 0, 128), [[-1, 128]], OP.is_equal, 0.0, 0, 1)
+    iota(("it2",), [[16, 64]], ST, 0)
+
+    act(("warm",), ("ones", 0, 8), AF.Sigmoid)
+    for a in (0, 1024):
+        act(("R", a, a + 1024), ("ones",), AF.Copy, scale=-1.0)
+    for a in range(0, ZS, 1024):
+        act(("w2", a, a + 1024), ("ones",), AF.Copy, scale=0.0)
+
+    fill(("C",), 0.0)
+    fill(("w1", 0, 3072), 0.0)
+    for q in range(8):
+        tc("v", ("C", 16 * q, 16 * q + 129 * 15 + 1, 129), ("B", 16 * q, 16 * q + 16))
+    fill(("one32",), 1.0)
+    ts(("itp",), ("itp",), 15, OP.bitwise_and)
+    tt(("t512",), ("it3",), ("itp", 0, 32), OP.add)
+    fill(("comp", 0, CAP), 255)
+    tc("v", ("snd16",), ("snd32",))
+    fill(("w1", 3072, ZV), 0.0)
+
+    gat("v", ("xsend",), ("xw", 0, P), ("snd16",))
+    send("x", "xsend", "xw", P, 1)
+    sel(("R",), ("R",), [[-1, 128], [0, 16]], OP.is_equal, 0.0, 0, 1)
+    iota(("cst",), [[0, 1024]], 30, 0)
+    iota(("io384",), [[1, NB]], -NB // 2, 0)
+    iota(("bw",), [[0, P]], NB // 2, 0)
+    sums(("psA", 0, 32), [(cmat(r), ("sdrep", r, BS, 16)) for r in range(16)])
     pack(0)
     lists(0)
-    slots(0)
-    fill(("cst",), 30.0)
-    fill(("bw",), float(NB // 2))
-    sca(("bw",), ("snd16",), ("io384",))
-    for r in range(16):
-        mm(("psB", 0, 64), cmat(r), ("bw", BS + r, 3 * BS, 16), r == 0, r == 15)
-    ts(("binv",), ("psB", 0, 64), 1.0 / 16, OP.mult, float(NB // 2), OP.add)
-    fill(("L0", NB, 400), 0.0)
-    fill(("L1", NB, 400), 0.0)
+    streams["f0"]["Q"]()
+    tt(("trash",), ("it2",), ("itp",), OP.add)
     need("y", [("rs_x", total["rs_x"])])
+    dma("y", "zz", [(T.w2[:, ZS:ST], T.w2[:, 0:ST - ZS])], [("w2", 0, ST - ZS)], [("w2", ZS, ST)])
+    dma("y", "zv", [(T.w1[:, ZV:ST], T.w1[:, 0:ST - ZV])], [("w1", 0, ST - ZV)], [("w1", ZV, ST)])
     dma("y", "ya", [(T.ya[:, YO:YO + P], T.y0[:, :])], [], [("ya", YO, YO + P)])
     dma("y", "yb", [(T.yb[:, YO:YO + P], T.y0[:, :])], [], [("yb", YO, YO + P)])
 
-    fwd_match(0, {}, True)
-    flags_out(0)
+    play("out0")
     own_flags(1)
+    for s in range(3):
+        ts(("vs%d" % s,), ("t512",), float(512 * s - 256), OP.add)
     pack(1)
+    sca(("bw",), ("snd16",), ("io384",))
+    sums(("psB", 0, 64), [(cmat(r), ("bw", BS + r, 3 * BS, 16)) for r in range(16)])
+    slots(0)
+    ts(("binv",), ("psB", 0, 64), 1.0 / 16, OP.mult, float(NB // 2), OP.add)
+    fill(("L0", NB, 400), 0.0)
     fill(("comp", 0, CAP), 255)
-    fill(("d0",), 0.0)
-    fill(("d0", 0, 1024, 16), 191.0)
     gat("s", ("ysend",), ("ya", YO, YO + P), ("snd16",))
     their_flags(1)
     need("g", [("rs_f0", total["rs_f0"])])
     send("y", "ysend", "ya", YO + P, 1)
     lists(1)
-    fwd_match(1, {"g2": lambda: slots(1)}, True)
-    flags_out(1)
+    streams["f1"]["Q"]()
+    play("out1")
     own_flags(2)
+    slots(1)
     pack(2)
     fill(("comp", 0, CAP), 255)
+    fill(("L1", NB, 400), 0.0)
+    fill(("d0",), 0.0)
+    fill(("d0", 0, 1024, 16), 191.0)
+    ts(("hI",), ("ident",), 0.5, OP.mult)
+    ts(("qI",), ("ident",), -0.25, OP.mult)
     fill(("mw", 0, CAP), 1.0)
     fill(("mw", CAP, CAP + 1536), 0.0)
     fill(("memblk",), 0.0)
     ts(("snd2i",), ("snd32",), 2, OP.mult)
     tc("v", ("snd2",), ("snd2i",))
-    members(0)
-    members(1)
+    streams["f0"]["M"]()
+    streams["f1"]["M"]()
     their_flags(2)
     lists(2)
-    take_xt(2)
-    slots(2)
-    bwd(2, "ya", "yb", None)
-    border_y("b2", "yb")
-    dma("y", "cy", [(T.ya[:, YO + 2 * BS:YO + 3 * BS], T.yb[:, YO + 2 * BS:YO + 3 * BS])],
-        [("yb", YO + 2 * BS, YO + 3 * BS)], [("ya", YO + 2 * BS, YO + 3 * BS)])
-    dma("y", "o2", [(T.yv[:, 2 * BS:3 * BS], T.yb[:, YO + 2 * BS:YO + 3 * BS])], [("yb", YO + 2 * BS, YO + 3 * BS)], [])
-    fwd_match(2, {}, False)
-    members(2)
-    dma("y", "blm", [(T.memblk[b::16, 0:min(336, 1536 - 336 * b)], T.memrep[b::16, 336 * b:min(1536, 336 * b + 336)]) for b in range(5)],
-        [("memrep",)], [("memblk",)])
-    bwd(1, "yb", "ya", None)
-    border_y("b1", "ya")
-    dma("y", "o1", [(T.yv[:, BS:2 * BS], T.ya[:, YO + BS:YO + 2 * BS])], [("ya", YO + BS, YO + 2 * BS)], [])
-    flags_out(2)
-    dma("y", "bl2", [(T.w2blk[b::16, :], T.w2[b::16, 672 * b:672 * b + 672]) for b in range(16)], [("w2", 0, 2 * P)], [("w2blk",)])
-
-    def last_flags():
-        w, o, i = ("w1", 0, 2 * P), ("tmpR",), ("L2", 0, NB)
-        op("v", lambda: g.vector.tensor_tensor(ap(o), ap(w).indirect(ap(("snd2",))), ap(i), OP.add), [w, i, ("snd2",)], [o])
-        sca(w, ("snd2",), o)
-        dma("y", "bl1", [(T.w1blk[b::16, :], T.w1[b::16, 672 * b:672 * b + 672]) for b in range(16)], [w], [("w1blk",)])
-    bwd(0, "ya", "yb", last_flags)
+    play("back2a") if "back2a" in SCHED else slots(2)
+    play("back2")
+    play("gap1")
+    play("back1")
+    play("gap0")
+    play("back0")
     dma("y", "o0", [(T.yv[:, 0:BS], T.yb[:, YO:YO + BS])], [("yb", YO, YO + BS)], [])
-    tc("s", ("w2bb",), ("w2blk",))
-    parts = [("sdblk",), ("w1blk", 0, 672, 2), ("w1blk", 1, 672, 2), ("w2bb", 0, 672, 2), ("w2bb", 1, 672, 2)]
-    for k, r in enumerate(parts):
-        mm(("psB", 0, 336), ("ident",), r, k == 0, k == len(parts) - 1)
-    ts(("yfl",), ("psB", 0, 336), 0.25, OP.is_gt)
-    tt(("yfb",), ("yfl",), ("memblk",), OP.add)
+    i = ("ident",)
+    sums(("psB", 0, 336), [(i, ("sdblk",)), (i, ("w2bb", 0, 672, 2)), (i, ("w2bb", 1, 672, 2)), (i, ("w1blk", 0, 672, 2)), (i, ("w1blk", 1, 672, 2))])
+    ts(("psB", 0, 336), ("psB", 0, 336), 0.25, OP.is_gt)
+    tt(("yfb",), ("psB", 0, 336), ("memblk",), OP.add)
     dma("s", "of", [(T.yf[:, :], T.yfb[:, :])], [("yfb",)], [])
-    need("g", [(s, n) for s, n in total.items()])
+    need("g", list(total.items()))
     for s, n in total.items():
         if s != "qg" and known["g"].get(s, 0) < n:
             g.wait_ge(T.sem[s], n)

from concourse.bass import DstId, RemoteDMATransfer
from concourse.mybir import AluOpType as OP, ActivationFunctionType as AF

P, PL, NB, BS, CAP, BK = 5376, 5760, 384, 512, 256, 128
ST = 2 * PL
WW = ST + 1024
ZV, ZS = 6144, 9216
BIG = 1023.0
YO = CAP
SPLITF, SPLITB = (40, 40, 40, 40), (30, 30, 34, 44)

BT = " G2 X1 N0 L0 A1 G3 N1 C0 X2 L1 A2 P0 N2 C1 X3 L2 A3 "
BE = " P1 B0 N3 C2 H L3 D0 P2 C3 P3 B1 D1 U "
FT = " G0 T c G1 X0 A0 G2 X1 L0 A1 G3 C0 X2 L1 A2 P0 C1 X3 L2 A3 P1 C2 S0-4 S4-8 P2 V8-10 L3 C3 V10-12 P3 V12-16 F"
SCHED = {
    "out0": "f0" + FT,
    "out1": "f1" + FT,
    "back2": "b2 G0 T c G1 X0 A0" + BT + "; f2 g0 g1 ; b2" + BE + "Y",
    "gap1": "f2 Q v0 v1 X0 A0 G2 X1 L0 A1 G3 C0 X2 L1 A2 P0 C1 X3 ; b1 g0 ; f2 L2 A3 P1 C2 ; b1 v0 g1 ; f2 L3 P2 C3 ; b1 v1 ; f2 P3",
    "back1": "b1 X0 A0" + BT + "; f2 S0-2 ; b1" + BE + "Y",
    "gap0": "f2 S2-6 S6-8 V8-12 V12-16 F M",
    "back0": "b0 G0 G1 X0 A0" + BT + "W R" + BE,
}

SCRATCH = {
    "xw": ("sbuf", [128, PL], "bfloat16"),
    "ya": ("sbuf", [128, YO + PL], "bfloat16"), "yb": ("sbuf", [128, YO + PL], "bfloat16"),
    "cdt": ("sbuf", [128, 1536], "int32"), "comp": ("sbuf", [128, 1024], "int32"),
    "snd32": ("sbuf", [128, 24], "int32"), "snd16": ("sbuf", [128, 24], "uint16"), "snd2": ("sbuf", [128, 24], "uint16"),
    "snd2i": ("sbuf", [128, 24], "int32"),
    "ci": ("sbuf", [128, 256], "int32"), "xi": ("sbuf", [128, 256], "int32"), "vt": ("sbuf", [128, 256], "int32"),
    "cf": ("sbuf", [128, 4096], "bfloat16"), "cb": ("sbuf", [128, 4096], "bfloat16"),
    "scn": ("sbuf", [128, 4096], "bfloat16"),
    "d0": ("sbuf", [128, 1024], "bfloat16"), "mt": ("sbuf", [128, 256], "bfloat16"), "hi": ("sbuf", [128, 256], "int32"),
    "vo": ("sbuf", [128, 256], "uint16"), "trash": ("sbuf", [128, 64], "float32"),
    "w1": ("sbuf", [128, WW], "bfloat16"), "w2": ("sbuf", [128, WW], "float32"),
    "ones": ("sbuf", [128, 1024], "bfloat16"), "cst": ("sbuf", [128, 1024], "float32"),
    "C": ("sbuf", [128, 2048], "bfloat16"), "R": ("sbuf", [128, 2048], "bfloat16"), "neg": ("sbuf", [128, 128], "bfloat16"),
    "ident": ("sbuf", [128, 128], "bfloat16"), "B": ("sbuf", [128, 128], "bfloat16"), "A1": ("sbuf", [128, 128], "bfloat16"),
    "hI": ("sbuf", [128, 128], "bfloat16"), "qI": ("sbuf", [128, 128], "bfloat16"),
    "sdrep": ("sbuf", [128, 512], "bfloat16"), "sdblk": ("sbuf", [128, 336], "bfloat16"),
    "L0": ("sbuf", [128, 400], "bfloat16"), "L1": ("sbuf", [128, 400], "bfloat16"), "L2": ("sbuf", [128, 400], "bfloat16"),
    "Lg": ("sbuf", [128, 512], "bfloat16"), "fsend": ("sbuf", [128, NB], "bfloat16"),
    "xsend": ("sbuf", [128, NB], "bfloat16"), "ysend": ("sbuf", [128, NB], "bfloat16"),
    "bw": ("sbuf", [128, P], "bfloat16"), "io384": ("sbuf", [128, NB], "bfloat16"), "binv": ("sbuf", [128, 64], "uint16"),
    "c2b": ("sbuf", [128, 768], "bfloat16"), "c2w": ("sbuf", [128, 1024], "bfloat16"),
    "tlb": ("sbuf", [128, 1], "bfloat16"), "warm": ("sbuf", [128, 8], "float32"),
    "flw": ("sbuf", [128, 32], "bfloat16"), "one32": ("sbuf", [128, 32], "float32"), "sc32": ("sbuf", [128, 32], "float32"),
    "pp": ("sbuf", [128, 32], "float32"), "sl": ("sbuf", [128, 32], "float32"), "sl16": ("sbuf", [128, 32], "uint16"),
    "zz": ("sbuf", [128, 32], "float32"), "t512": ("sbuf", [128, 32], "float32"),
    "itp": ("sbuf", [128, 64], "int32"), "it2": ("sbuf", [128, 64], "int32"), "it3": ("sbuf", [128, 32], "int32"),
    "mw": ("sbuf", [128, CAP + 1536], "bfloat16"), "memrep": ("sbuf", [128, 1536], "bfloat16"),
    "memblk": ("sbuf", [128, 336], "bfloat16"), "w1blk": ("sbuf", [128, 672], "bfloat16"),
    "w2blk": ("sbuf", [128, 672], "float32"), "w2bb": ("sbuf", [128, 672], "bfloat16"),
    "tmpR": ("sbuf", [128, NB], "bfloat16"), "yfb": ("sbuf", [128, 336], "bfloat16"),
    "psd0": ("psum", [128, 1024], "float32"), "psd1": ("psum", [128, 1024], "float32"),
    "cnt0": ("psum", [128, 512], "float32"), "cnt1": ("psum", [128, 512], "float32"),
    "psA": ("psum", [128, 512], "float32"), "psB": ("psum", [128, 512], "float32"),
}
for _s in range(3):
    SCRATCH["c16_%d" % _s] = ("sbuf", [128, 256], "uint16")
    SCRATCH["xm%d" % _s] = ("sbuf", [128, 256], "bfloat16")
    SCRATCH["xT%d" % _s] = ("sbuf", [128, 256], "bfloat16")
    SCRATCH["sb16_%d" % _s] = ("sbuf", [128, 32], "uint16")
    SCRATCH["vs%d" % _s] = ("sbuf", [128, 32], "float32")
    SCRATCH["ab%d" % _s] = ("sbuf", [128, 1024], "bfloat16")
    SCRATCH["nr%d" % _s] = ("sbuf", [128, 1024], "bfloat16")

_EX = ["x", "f0", "y", "f1", "b2", "f2", "b1"]
_DM = ["snd", "xa", "xb", "tl", "sd", "cd0", "cd1", "sk", "zz", "zv", "ya", "yb", "bl1", "bl2", "blm", "cy", "o2", "o1",
       "o0", "of"]
SEMAPHORES = ["qv", "qs", "qt", "qg"] + ["ls_" + e for e in _EX] + ["rs_" + e for e in _EX] + ["d_" + d for d in _DM]


def rank_program(g, core, T, topo):
    rank = T.rank_of(core)
    if rank is None:
        return
    nr_ranks = len(T.cores)
    eng = {"v": g.vector, "s": g.scalar, "t": g.tensor, "g": g, "y": g.sync}
    known = {q: {} for q in eng}
    clock = {}
    total = {}
    recs = {}

    def width(n):
        return SCRATCH[n][1][1]

    def reg(r):
        return r[0], (r[1] if len(r) > 1 else 0), (r[2] if len(r) > 2 else width(r[0]))

    def is_ps(n):
        return SCRATCH[n][0] == "psum"

    def ap(r):
        n, a, b = reg(r)
        if len(r) > 3:
            return T[n][:, a:b:r[3]]
        return T[n][:, a:b]

    def need(q, evs):
        best = {}
        for sem, n in evs:
            if known[q].get(sem, 0) < n and best.get(sem, 0) < n:
                best[sem] = n
        for sem in list(best):
            n = best[sem]
            if any(o != sem and clock[(o, m)].get(sem, 0) >= n for o, m in best.items()):
                del best[sem]
        for sem, n in best.items():
            eng[q].wait_ge(T.sem[sem], n)
            for k, m in clock[(sem, n)].items():
                if known[q].get(k, 0) < m:
                    known[q][k] = m

    def deps(q, R, W):
        evs = []
        for r, w in [(r, is_ps(r[0])) for r in R] + [(r, True) for r in W]:
            n, a, b = reg(r)
            if is_ps(n):
                a, b = 0, width(n)
            for c0, c1, iw, qq, ev in recs.get(n, []):
                if c0 < b and a < c1 and (w or iw) and not (q == "t" and qq == "t"):
                    evs.append(ev)
        return evs

    def note(q, R, W, ev):
        for r in W:
            n, a, b = reg(r)
            if is_ps(n):
                a, b = 0, width(n)
                recs[n] = [e for e in recs.get(n, []) if q == "t" and e[3] == "t"]
            elif len(r) <= 3:
                recs[n] = [e for e in recs.get(n, []) if not (a <= e[0] and e[1] <= b)]
            recs.setdefault(n, []).append((a, b, True, q, ev))
        for r in R:
            n, a, b = reg(r)
            if is_ps(n):
                recs[n] = [(0, width(n), True, q, ev)]
            else:
                recs.setdefault(n, []).append((a, b, False, q, ev))

    def event(q, sem, n):
        total[sem] = total.get(sem, 0) + n
        ev = (sem, total[sem])
        clock[ev] = dict(known[q])
        clock[ev][sem] = total[sem]
        return ev

    def op(q, fn, R, W):
        need(q, deps(q, R, W))
        sem = "q" + q
        fn().then_inc(T.sem[sem], 1)
        note(q, R, W, event(q, sem, 1))

    def dma(q, name, pairs, R, W):
        need(q, deps(q, R, W))
        for o, i in pairs:
            eng[q].dma_start(o, i).then_inc(T.sem["d_" + name], 16)
        note(q, R, W, event(q, "d_" + name, 16 * len(pairs)))

    def act(o, i, f, **k):
        op("s", lambda: g.scalar.activation(ap(o), ap(i), f, **k), [i], [o])

    def tc(q, o, i):
        if q == "v":
            op("v", lambda: g.vector.tensor_copy(ap(o), ap(i)), [i], [o])
        else:
            act(o, i, AF.Copy)

    def gat(q, o, win, off):
        if q == "v":
            op("v", lambda: g.vector.tensor_copy(ap(o), ap(win).indirect(ap(off))), [win, off], [o])
        else:
            op("s", lambda: g.scalar.activation(ap(o), ap(win).indirect(ap(off)), AF.Copy), [win, off], [o])

    def sca(win, off, i):
        op("v", lambda: g.vector.tensor_copy(ap(win).indirect(ap(off)), ap(i)), [i, off], [win])

    def tt(o, a, b, f):
        op("v", lambda: g.vector.tensor_tensor(ap(o), ap(a), ap(b), f), [a, b], [o])

    def ts(o, a, s1, f1, s2=None, f2=None):
        if f2 is None:
            op("v", lambda: g.vector.tensor_scalar(ap(o), ap(a), s1, None, f1), [a], [o])
        else:
            op("v", lambda: g.vector.tensor_scalar(ap(o), ap(a), s1, s2, f1, f2), [a], [o])

    def fill(o, c):
        op("v", lambda: g.vector.memset(ap(o), c), [], [o])

    def mm(o, l, r, start, stop):
        op("t", lambda: g.tensor.matmul(ap(o), ap(l), ap(r), start, stop), [l, r], [o])

    def sums(o, terms):
        for k, (l, r) in enumerate(terms):
            mm(o, l, r, k == 0, k == len(terms) - 1)

    def sel(o, i, pattern, cmp, fl, base, cm):
        op("g", lambda: g.affine_select(ap(o), ap(i), pattern, cmp, fl, base, cm), [i], [o])

    def iota(o, pattern, base, cm):
        if SCRATCH[o[0]][2] == "int32":
            op("g", lambda: g.iota(ap(o), pattern, base, cm), [], [o])
        else:
            op("g", lambda: g.iota(ap(o), pattern, base, cm, allow_small_or_imprecise_dtypes=True), [], [o])

    def send(name, src, dst, col, sign):
        need("g", deps("g", [(src,)], []))
        trs, cnt, at = [], 0, 0
        for d in range(1, nr_ranks):
            to = T.cores[(rank + sign * d) % nr_ranks]
            es = topo.engines(core, to)
            n = len(es) // 4
            a, b = topo.chip(core), topo.chip(to)
            if topo.mates(a, b) or topo.same_plane(a, b):
                mine = es[at:at + n]
                at += n
            else:
                mine = es[2 * n:]
            rid, pid, _ = topo.addr(to)
            c0 = col + (d - 1) * BK
            trs.append(RemoteDMATransfer(dst_ids=[DstId(rid=rid, pnc=pid)], dma_engine_mask=sum(1 << e for e in mine),
                                         remote_sem=T.sem["rs_" + name], src=T[src][:, (d - 1) * BK:d * BK],
                                         dst=T[dst][:, c0:c0 + BK]))
            cnt += len(mine)
        g.remote_dma_fused(trs, local_sem=T.sem["ls_" + name])
        note("g", [(src,)], [], event("g", "ls_" + name, cnt))
        total["rs_" + name] = cnt
        ev = ("rs_" + name, cnt)
        clock[ev] = {"rs_" + name: cnt}
        recs[dst] = [e for e in recs.get(dst, []) if not (col <= e[0] and e[1] <= col + NB)]
        recs[dst].append((col, col + NB, True, "r", ev))

    def cmat(r):
        return ("C", 128 * r, 128 * r + 128)

    def pack(s):
        r = ("cdt", BS * s, BS * s + BS)
        ts(r, r, 256, OP.mult)
        tt(r, r, ("xw", BS * s, BS * s + BS), OP.add)

    def offsets(s, a, b):
        ts(("ci", a, b), ("comp", a, b), 9, OP.arith_shift_right)
        tc("v", ("c16_%d" % s, a, b), ("ci", a, b))

    def lists(s):
        ts(("flw",), ("psA", 0, 32), 0.25, OP.is_gt)
        mm(("psB", 0, 32), ("B",), ("flw",), True, True)
        mm(("psB", 32, 64), ("A1",), ("flw",), True, True)
        op("v", lambda: g.vector.tensor_tensor_scan(ap(("sc32",)), ap(("one32",)), ap(("psB", 0, 32)), BIG, OP.mult, OP.add),
           [("one32",), ("psB", 0, 32)], [("sc32",)])
        tt(("pp",), ("psB", 32, 64), ("sc32",), OP.add)
        tt(("sl",), ("pp",), ("t512",), OP.min)
        tc("v", ("sl16",), ("sl",))
        sca(("comp",), ("sl16",), ("cdt", BS * s, BS * s + BS))
        offsets(s, 0, 128)
        ts(("xi",), ("comp", 0, CAP), 255, OP.bitwise_and)
        tc("v", ("xm%d" % s,), ("xi",))
        for k in range(2):
            mm(("psA", 128 * k, 128 * k + 128), ("xm%d" % s, 128 * k, 128 * k + 128), ("ident",), True, True)

    def slots(s):
        ts(("zz",), ("pp",), 255.5, OP.is_gt, 8192.0, OP.mult)
        tt(("zz",), ("pp",), ("zz",), OP.add)
        tt(("zz",), ("zz",), ("vs%d" % s,), OP.min)
        tc("v", ("sb16_%d" % s,), ("zz",))

    def own_flags(s):
        a = 2 * BS * s
        tc("s", ("c2w",), ("w2", a, a + 1024))
        for n, lo, hi in (("w1", a, a + 1024), ("c2w", 0, 1024)):
            for r in range(16):
                for b in range(2):
                    mm(("psA", 0, 32), cmat(r), (n, lo + 2 * r + b, hi, 32), n == "w1" and r + b == 0, False)

    def their_flags(s):
        k = 32 * (s - 1)
        w = ("L%d" % (s - 1),)
        gat("s", ("Lg", 256, 512), w, ("binv", k + 16, k + 32))
        gat("v", ("Lg", 0, 256), w, ("binv", k, k + 16))
        for r in range(16):
            mm(("psA", 0, 32), cmat(r), ("Lg", r, 512, 16), False, r == 15)

    def stream(name):
        s, out = int(name[1]), name[0] == "f"
        wn, w0, cand, split = ("xw", 0, "cf", SPLITF) if out else (("ya", "yb")[s % 2], YO, "cb", SPLITB)
        ot = ("yb", "ya")[s % 2]
        win, off = (wn, w0, w0 + PL), "c16_%d" % s

        def gs(c):
            k, j, n = 64 * c, 1024 * c, split[c]
            gat("s", (cand, j + 16 * n, j + 1024), win, (off, k + n, k + 64))

        def gv(c):
            k, j, n = 64 * c, 1024 * c, split[c]
            gat("v", (cand, j, j + 16 * n), win, (off, k, k + n))

        def G(c):
            gs(c)
            gv(c)

        def X(c):
            ps, hf = "psd%d" % (c % 2), c // 2
            for b in range(2):
                q = (2 * c + b) % 4
                mm((ps, 512 * b, 512 * b + 512), ("xT%d" % s, 128 * hf, 128 * hf + 128), ("R", 512 * q, 512 * q + 512), True, False)
            for b in range(2):
                j = 1024 * c + 512 * b
                mm((ps, 512 * b, 512 * b + 512), ("ident",), (cand, j, j + 512), False, True)

        def A(c):
            act(("ab%d" % (c % 3),), ("psd%d" % (c % 2),), AF.Abs)

        def L(c):
            o, i = ("nr%d" % (c % 3),), ("ab%d" % (c % 3),)
            op("v", lambda: g.vector.tensor_scalar(ap(o), ap(i), ap(("tlb",)), None, OP.is_le), [i, ("tlb",)], [o])

        def cn(c, at=0):
            k = at + 64 * (c // 2)
            return ("cnt%d" % (c % 2), k, k + 64)

        def C(c):
            sums(cn(c), [(cmat(i), ("nr%d" % (c % 3), i, 1024, 16)) for i in range(16)])

        def Pt(c):
            r = (64 * c, 64 * c + 64)
            if out:
                m = cn(c, 256)
                ts(m, cn(c), 8.5, OP.is_lt, 30000.0, OP.mult)
                tt(m, m, ("trash",), OP.min)
                tt(m, m, ("vt",) + r, OP.max)
                tc("v", ("vo",) + r, m)
            else:
                ts(("mt",) + r, cn(c), 8.5, OP.is_ge)

        def S(a, b):
            w, o, i = ("w2",), ("vo", 16 * a, 16 * b), ("cst", 0, 256 * (b - a))
            op("s", lambda: g.scalar.activation(ap(w).indirect(ap(o)), ap(i), AF.Sigmoid), [o, i], [w])

        def V(a, b):
            sca(("w1",), ("vo", 16 * a, 16 * b), ("ones", 0, 256 * (b - a)))

        def F():
            tc("s", ("c2b",), ("w2", 2 * P, ST))
            i = ("ident",)
            sums(("psB", 0, NB), [(i, ("c2b", 0, 768, 2)), (i, ("c2b", 1, 768, 2)), (i, ("w1", 2 * P, ST, 2)), (i, ("w1", 2 * P + 1, ST, 2))])
            tc("v", ("fsend",), ("psB", 0, NB))
            send("f%d" % s, "fsend", "L%d" % s, 0, -1)

        def N(c):
            i, o = ("cb", 1024 * c, 1024 * c + 1024), ("scn", 1024 * c, 1024 * c + 1024)
            op("v", lambda: g.vector.tensor_tensor_scan(ap(o), ap(("d0",)), ap(i), 191.0, OP.max, OP.min), [i, ("d0",)], [o])

        def H():
            sums(("psB", 0, 256), [(("hI",), ("xm%d" % s,)), (("qI",), ("ones", 0, 256)), (("hI",), ("scn", 15, 4096, 16))])
            tc("v", ("hi",), ("psB", 0, 256))

        def Bm(k):
            mm(("psA", 128 * k, 128 * k + 128), ("B",), ("mt", 128 * k, 128 * k + 128), True, True)

        def D(k):
            r = (128 * k, 128 * k + 128)
            m = ("psA", 256 + 128 * k, 384 + 128 * k)
            ts(m, ("psA",) + r, 1.5, OP.is_ge, 255.0, OP.mult)
            tt((wn,) + r, ("hi",) + r, m, OP.max)

        def U():
            a = YO + BS * s
            gat("s", (ot, a + 256, a + 512), (wn, 0, YO + P), ("sb16_%d" % s, 16, 32))
            gat("v", (ot, a, a + 256), (wn, 0, YO + P), ("sb16_%d" % s, 0, 16))

        def Y():
            w = (ot, YO, YO + P)
            gat("s", ("ysend", 192, 384), w, ("snd16", 12, 24))
            gat("v", ("ysend", 0, 192), w, ("snd16", 0, 12))
            send("b%d" % s, "ysend", ot, YO + P, 1)
            r = (YO + BS * s, YO + BS * s + BS)
            dma("y", "o%d" % s, [(T.yv[:, BS * s:BS * s + BS], ap((ot,) + r))], [(ot,) + r], [])
            if s == 2:
                dma("y", "cy", [(ap((wn,) + r), ap((ot,) + r))], [(ot,) + r], [(wn,) + r])

        def Tk():
            tc("s", ("xT%d" % s,), ("psA", 0, 256))

        def ck():
            offsets(s, 128, 256)

        def Q():
            ts(("vt",), ("comp", 0, CAP), 8, OP.arith_shift_right)

        def R():
            w, o, i = ("w1", 0, 2 * P), ("tmpR",), ("L2", 0, NB)
            op("v", lambda: g.vector.tensor_tensor(ap(o), ap(w).indirect(ap(("snd2",))), ap(i), OP.add), [w, i, ("snd2",)], [o])
            sca(w, ("snd2",), o)
            dma("y", "bl1", [(T.w1blk[b::16, :], T.w1[b::16, 672 * b:672 * b + 672]) for b in range(16)], [w], [("w1blk",)])

        def M():
            gat("s", ("memrep", BS * s, BS * s + BS), ("mw",), ("sb16_%d" % s,))
            if s == 2:
                dma("y", "bl2", [(T.w2blk[b::16, :], T.w2[b::16, 672 * b:672 * b + 672]) for b in range(16)], [("w2", 0, 2 * P)], [("w2blk",)])
                dma("y", "blm", [(T.memblk[b::16, 0:min(336, 1536 - 336 * b)], T.memrep[b::16, 336 * b:min(1536, 336 * b + 336)])
                                 for b in range(5)], [("memrep",)], [("memblk",)])

        def W():
            tc("s", ("w2bb",), ("w2blk",))
        return {"G": G, "g": gs, "v": gv, "X": X, "A": A, "L": L, "C": C, "P": Pt, "S": S, "V": V, "F": F, "N": N, "H": H,
                "B": Bm, "D": D, "U": U, "Y": Y, "T": Tk, "c": ck, "Q": Q, "R": R, "M": M, "W": W}

    streams = {n: stream(n) for n in ("f0", "f1", "f2", "b2", "b1", "b0")}

    def play(key):
        for part in SCHED[key].split(";"):
            words = part.split()
            for w in words[1:]:
                streams[words[0]][w[0]](*[int(a) for a in w[1:].split("-") if a])

    h = P // 2
    dma("y", "xa", [(T.xw[:, 0:h], T.x[:, 0:h])], [], [("xw", 0, h)])
    dma("s", "snd", [(T.snd32[:, :], T.snd[:, :])], [], [("snd32",)])
    dma("s", "xb", [(T.xw[:, h:P], T.x[:, h:P])], [], [("xw", h, P)])
    fill(("sdrep",), 0.0)
    fill(("ones",), 1.0)
    fill(("neg",), -1.0)
    fill(("sdblk",), 0.0)
    dma("y", "sd", [(T.sdrep[0::16, :], T.sd[:, :])], [], [("sdrep",)])
    dma("y", "cd0", [(T.cdt[:, 0:BS], T.cd[:, 0:BS])], [], [("cdt", 0, BS)])
    dma("y", "tl", [(T.tlb[:, :], T.tl[:, :])], [], [("tlb",)])
    dma("y", "sk", [(T.sdblk[0::16, :], T.sd[:, 0:336]), (T.sdblk[1::16, 0:BS - 336], T.sd[:, 336:BS])], [], [("sdblk",)])
    dma("y", "cd1", [(T.cdt[:, BS:3 * BS], T.cd[:, BS:3 * BS])], [], [("cdt", BS, 3 * BS)])

    sel(("B",), ("ones", 0, 128), [[-16, 8], [0, 16]], OP.is_ge, 0.0, 0, 1)
    sel(("B",), ("B",), [[16, 8], [0, 16]], OP.is_ge, 0.0, 15, -1)
    iota(("itp",), [[0, 64]], 0, 1)
    iota(("it3",), [[16, 32]], BS, 0)
    sel(("A1",), ("neg",), [[16, 8], [0, 16]], OP.is_ge, 0.0, 15, -1)
    sel(("A1",), ("A1",), [[-1, 128]], OP.is_gt, 0.0, 0, 1)
    sel(("A1",), ("A1",), [[-1, 128]], OP.not_equal, -(BIG + 1), 0, 1)
    sel(("ident",), ("ones", 0, 128), [[-1, 128]], OP.is_equal, 0.0, 0, 1)
    iota(("it2",), [[16, 64]], ST, 0)

    act(("warm",), ("ones", 0, 8), AF.Sigmoid)
    for a in (0, 1024):
        act(("R", a, a + 1024), ("ones",), AF.Copy, scale=-1.0)
    for a in range(0, ZS, 1024):
        act(("w2", a, a + 1024), ("ones",), AF.Copy, scale=0.0)

    fill(("C",), 0.0)
    fill(("w1", 0, 3072), 0.0)
    for q in range(8):
        tc("v", ("C", 16 * q, 16 * q + 129 * 15 + 1, 129), ("B", 16 * q, 16 * q + 16))
    fill(("one32",), 1.0)
    ts(("itp",), ("itp",), 15, OP.bitwise_and)
    tt(("t512",), ("it3",), ("itp", 0, 32), OP.add)
    fill(("comp", 0, CAP), 255)
    tc("v", ("snd16",), ("snd32",))
    fill(("w1", 3072, ZV), 0.0)

    gat("v", ("xsend",), ("xw", 0, P), ("snd16",))
    send("x", "xsend", "xw", P, 1)
    sel(("R",), ("R",), [[-1, 128], [0, 16]], OP.is_equal, 0.0, 0, 1)
    iota(("cst",), [[0, 1024]], 30, 0)
    iota(("io384",), [[1, NB]], -NB // 2, 0)
    iota(("bw",), [[0, P]], NB // 2, 0)
    sums(("psA", 0, 32), [(cmat(r), ("sdrep", r, BS, 16)) for r in range(16)])
    pack(0)
    lists(0)
    streams["f0"]["Q"]()
    tt(("trash",), ("it2",), ("itp",), OP.add)
    need("y", [("rs_x", total["rs_x"])])
    dma("y", "zz", [(T.w2[:, ZS:ST], T.w2[:, 0:ST - ZS])], [("w2", 0, ST - ZS)], [("w2", ZS, ST)])
    dma("y", "zv", [(T.w1[:, ZV:ST], T.w1[:, 0:ST - ZV])], [("w1", 0, ST - ZV)], [("w1", ZV, ST)])
    dma("y", "ya", [(T.ya[:, YO:YO + P], T.y0[:, :])], [], [("ya", YO, YO + P)])
    dma("y", "yb", [(T.yb[:, YO:YO + P], T.y0[:, :])], [], [("yb", YO, YO + P)])

    play("out0")
    own_flags(1)
    for s in range(3):
        ts(("vs%d" % s,), ("t512",), float(512 * s - 256), OP.add)
    pack(1)
    sca(("bw",), ("snd16",), ("io384",))
    sums(("psB", 0, 64), [(cmat(r), ("bw", BS + r, 3 * BS, 16)) for r in range(16)])
    slots(0)
    ts(("binv",), ("psB", 0, 64), 1.0 / 16, OP.mult, float(NB // 2), OP.add)
    fill(("L0", NB, 400), 0.0)
    fill(("comp", 0, CAP), 255)
    gat("s", ("ysend",), ("ya", YO, YO + P), ("snd16",))
    their_flags(1)
    need("g", [("rs_f0", total["rs_f0"])])
    send("y", "ysend", "ya", YO + P, 1)
    lists(1)
    streams["f1"]["Q"]()
    play("out1")
    own_flags(2)
    slots(1)
    pack(2)
    fill(("comp", 0, CAP), 255)
    fill(("L1", NB, 400), 0.0)
    fill(("d0",), 0.0)
    fill(("d0", 0, 1024, 16), 191.0)
    ts(("hI",), ("ident",), 0.5, OP.mult)
    ts(("qI",), ("ident",), -0.25, OP.mult)
    fill(("mw", 0, CAP), 1.0)
    fill(("mw", CAP, CAP + 1536), 0.0)
    fill(("memblk",), 0.0)
    ts(("snd2i",), ("snd32",), 2, OP.mult)
    tc("v", ("snd2",), ("snd2i",))
    streams["f0"]["M"]()
    streams["f1"]["M"]()
    their_flags(2)
    lists(2)
    play("back2a") if "back2a" in SCHED else slots(2)
    play("back2")
    play("gap1")
    play("back1")
    play("gap0")
    play("back0")
    dma("y", "o0", [(T.yv[:, 0:BS], T.yb[:, YO:YO + BS])], [("yb", YO, YO + BS)], [])
    i = ("ident",)
    sums(("psB", 0, 336), [(i, ("sdblk",)), (i, ("w2bb", 0, 672, 2)), (i, ("w2bb", 1, 672, 2)), (i, ("w1blk", 0, 672, 2)), (i, ("w1blk", 1, 672, 2))])
    ts(("psB", 0, 336), ("psB", 0, 336), 0.25, OP.is_gt)
    tt(("yfb",), ("psB", 0, 336), ("memblk",), OP.add)
    dma("s", "of", [(T.yf[:, :], T.yfb[:, :])], [("yfb",)], [])
    need("g", list(total.items()))
    for s, n in total.items():
        if s != "qg" and known["g"].get(s, 0) < n:
            g.wait_ge(T.sem[s], n)
